import numpy as np
import ml_dtypes


def mxq(x, axis, fmt="e4m3"):
    dtype, down = {"e4m3": (ml_dtypes.float8_e4m3fn, 7), "e5m2": (ml_dtypes.float8_e5m2, 14)}[fmt]
    v = np.moveaxis(np.asarray(x, np.float32).astype(ml_dtypes.bfloat16).astype(np.float64), axis, -1)
    blocks = v.reshape(v.shape[:-1] + (-1, 32))
    amax = np.abs(blocks).max(-1, keepdims=True)
    byte = np.maximum(np.where(amax > 0, np.frexp(amax)[1] - 1 + 127, 0) - down, 1)
    scale = np.exp2(byte - 127.0)
    codes = (blocks / scale).astype(np.float32).astype(dtype).astype(np.float64)
    return np.moveaxis((codes * scale).reshape(v.shape), -1, axis)


WIDE = False


def mx_kscale(k):
    if not WIDE:
        return np.ones(k)
    levels = np.array([10, -10, 5, -5, 0])
    if k % 512:
        return np.exp2(np.random.permutation(np.resize(levels, k // 32))).repeat(32)
    a = np.empty((k // 512, 16))
    for p in range(k // 512):
        a[p, :8] = np.random.permutation(np.resize(levels, 8))
        for g in range(8):
            far = levels[np.abs(levels - a[p, g]) >= 10]
            a[p, g + 8] = far[np.random.randint(len(far))]
    return np.exp2(a.ravel()).repeat(32)


def f64(x):
    return np.asarray(x).astype(np.float64)


def striped(idx):
    return np.tile(idx.reshape(-1, 16).T, (8, 1)).astype(np.uint16)


def unstriped(offs):
    return offs[:16].T.reshape(-1).astype(np.int64)


def pack_weight(w):
    k, n = w.shape
    w = f64(np.asarray(w, np.float32).astype(ml_dtypes.bfloat16)).reshape(k // 32, 32, n)
    amax = np.abs(w).max(1)
    byte = np.clip(np.where(amax > 0, np.frexp(amax)[1] - 1 + 127 - 7, 1), 1, 254)
    scaled = (w * np.exp2(127.0 - byte)[:, None, :]).reshape(k, n).astype(np.float32)
    words = np.ascontiguousarray(scaled.reshape(k // 512, 128, 4, n).transpose(0, 1, 3, 2)).astype(ml_dtypes.float8_e4m3fn).view(np.uint8)
    return words, np.ascontiguousarray(byte.astype(np.uint8).reshape(k // 512, 16, n))


def unpack_weight(words, scales):
    g, p, n, _ = words.shape
    vals = np.ascontiguousarray(words).view(ml_dtypes.float8_e4m3fn).astype(np.float64) * np.repeat(np.exp2(scales.astype(np.float64) - 127.0), 8, axis=1)[..., None]
    return vals.transpose(0, 1, 3, 2).reshape(g * 512, n)


def relu2(v):
    return np.maximum(v, 0.0) ** 2


K, T, E, C, N = 3072, 1024, 4, 256, 256


def by_expert(wq, xq):
    return np.concatenate([wq[e].T @ xq[:, e * C:(e + 1) * C] for e in range(E)], axis=1)


def setup_inputs():
    n = np.random.standard_normal
    s = mx_kscale(K)[:, None]
    packed = [pack_weight(m) for m in n((E, K, N)) / np.sqrt(K) / s[None]]
    return {
        "xT": (n((K, T)) * s).astype(np.float32),
        "w_words": np.stack([m[0] for m in packed]),
        "w_scales": np.stack([m[1] for m in packed]),
        "b": (0.3 * n((N, E))).astype(np.float32),
        "gate": np.tile(np.random.uniform(0.2, 1.0, E * C), (N, 1)).astype(np.float32),
        "offs": striped(np.random.permutation(T)[:E * C]),
    }


def reference(xT, w_words, w_scales, b, gate, offs):
    idx = unstriped(offs)
    xq = mxq(f64(xT)[:, idx], 0, "e4m3")
    w = np.stack([unpack_weight(w_words[e], w_scales[e]) for e in range(E)])
    y = by_expert(w, xq)
    y = relu2(y + np.repeat(f64(b), C, axis=1))
    out = np.zeros((N, T))
    out[:, idx] = f64(gate) * y
    return out

@@ -1,0 +1,159 @@
+from contextlib import ExitStack
+
+import concourse.mybir as mybir
+
+K, T, E, C, N = 3072, 1024, 4, 256, 256
+P = 128
+PASSES = K // 512
+FLOPS = 2 * K * N * E * C
+BYTES = 4 * K * T + E * K * N + E * K * N // 32 + 4 * N * E + 4 * E * C + 2 * P * (E * C // 16) + 4 * N * T
+
+F32 = mybir.dt.float32
+BF16 = mybir.dt.bfloat16
+I32 = mybir.dt.int32
+U32 = mybir.dt.uint32
+U16 = mybir.dt.uint16
+U8 = mybir.dt.uint8
+FP8X4 = mybir.dt.float8_e4m3fn_x4
+RELU = mybir.ActivationFunctionType.Relu
+SQUARE = mybir.ActivationFunctionType.Square
+MULT = mybir.AluOpType.mult
+
+H = 512
+WHOLE = [(0, 1024)]
+WHOLE = [(0, 1024)]
+WHOLE = [(0, 1024)]
+HALVES = [(0, 512), (512, 1024)]
+LOADS = [[(0, 256), (256, 512), (512, 1024)], HALVES, WHOLE, WHOLE, WHOLE, [(0, 512), (512, 768), (768, 1024)]]
+MIDS = [[(0, 512)], [(512, 928)]]
+MIDV = [[], [(928, 1024)]]
+SCALAR_PART = [[[(0, 256)], [(512, 704)]], [[(0, 512)], [(512, 832)]], MIDS, MIDS, MIDS, [[(0, 512)], [(512, 768), (768, 864)]]]
+VECTOR_PART = [[[(256, 512)], [(704, 1024)]], [[], [(832, 1024)]], MIDV, MIDV, MIDV, [[], [(864, 1024)]]]
+QUANT = [512, 512, 512, 512, 512, 256]
+
+
+def tile_routed_moe_kernel(tc, xT, w_words, w_scales, b, gate, offs, out):
+    nc = tc.nc
+    xv = xT.rearrange("(a p t) n -> a p t n", p=P, t=4)
+
+    with ExitStack() as ctx:
+        keep = ctx.enter_context(tc.tile_pool(name="keep", bufs=1))
+        rawp = ctx.enter_context(tc.tile_pool(name="rawp", bufs=4))
+        grpp = ctx.enter_context(tc.tile_pool(name="grpp", bufs=4))
+        psum = ctx.enter_context(tc.psum_pool(name="psum", bufs=1))
+
+        offsets = keep.tile([P, E * C // 16], U16, name="offsets")
+        bias = keep.tile([P, 2, E], F32, name="bias")
+        nc.scalar.dma_start(out=bias[:], in_=b.rearrange("(h p) e -> p h e", p=P))
+
+        qs = []
+        for g in range(2):
+            plane = keep.tile([P, T], U8, name=f"qs{g}", align_bytes=64)
+            nc.vector.memset(plane[:].bitcast(I32), 0)
+            qs.append(plane)
+        wsc = keep.tile([P, E * PASSES, N], U8, name="wsc", align_bytes=64)
+        nc.vector.memset(wsc[:].bitcast(I32), 0)
+
+        gw = {}
+        gs = {}
+
+        def gather_bytes(g, s):
+            t = keep.tile([P, H], U8, name=f"gs{g}{s}", align_bytes=64)
+            nc.vector.tensor_copy(t[:], qs[g][:].indirect(offsets[:, s * (H // 16):(s + 1) * (H // 16)]))
+            gs[g, s] = t
+
+        def gather_words(a, s, words):
+            t = keep.tile([P, H], U32, name=f"gw{a}{s}", align_bytes=64)
+            nc.vector.tensor_copy(t[:], words[:].indirect(offsets[:, s * (H // 16):(s + 1) * (H // 16)]))
+            gw[a, s] = t
+
+        wv = w_scales.rearrange("e a q n -> q (e a) n")
+        wt = {}
+
+        def load_scales():
+            for q in range(4):
+                nc.sync.dma_start(out=wsc[32 * q:32 * q + 4].bitcast(I32), in_=wv[4 * q:4 * q + 4].bitcast(I32))
+
+        def load_w(e):
+            w = keep.tile([P, PASSES, N], U32, name=f"w{e}", align_bytes=64)
+            nc.sync.dma_start(out=w[:].bitcast(I32), in_=w_words[e].rearrange("a p n r -> p a (n r)").bitcast(I32))
+            wt[e] = w
+
+        def find(pieces, lo, hi):
+            for plo, phi, tile in pieces:
+                if plo <= lo and hi <= phi:
+                    return tile[:, :, lo - plo:hi - plo]
+
+        for a in range(PASSES):
+            words = keep.tile([P, T], U32, name=f"qw{a}", align_bytes=64)
+            g, k = a // 4, 4 * (a % 4)
+            if a == 5:
+                load_scales()
+            pieces = []
+            for lo, hi in LOADS[a]:
+                raw = rawp.tile([P, 4, hi - lo], F32, name=f"raw{hi - lo}", bufs={1024: 3, 512: 4, 256: 4}[hi - lo], align_bytes=64)
+                nc.sync.dma_start(out=raw[:], in_=xv[a, :, :, lo:hi])
+                pieces.append((lo, hi, raw))
+                if a == 0 and lo == 0:
+                    nc.sync.dma_start(offsets[:], offs)
+            halves = []
+            for s in range(2):
+                grouped = grpp.tile([P, H, 4], BF16, name="grouped", align_bytes=64)
+                halves.append(grouped)
+                for engine, parts in ((nc.scalar.copy, SCALAR_PART[a][s]), (nc.vector.tensor_copy, VECTOR_PART[a][s])):
+                    for lo, hi in parts:
+                        engine(
+                            grouped[:, lo - s * H:hi - s * H, :].rearrange("p (c i) t -> p c t i", i=4),
+                            find(pieces, lo, hi).rearrange("p t (c i) -> p c t i", i=4),
+                        )
+            for s in range(2):
+                for lo in range(0, H, QUANT[a]):
+                    cols = slice(s * H + lo, s * H + lo + QUANT[a])
+                    nc.vector.quantize_mx(
+                        out=words[:, cols].bitcast(FP8X4),
+                        scales=qs[g][k:P, cols],
+                        in_=halves[s][:, lo:lo + QUANT[a], :].rearrange("p n t -> p (n t)"),
+                    )
+            for s in range(2):
+                if a in (3, 5):
+                    gather_bytes(g, s)
+                gather_words(a, s, words)
+
+        load_w(0)
+        load_w(1)
+        gate_sb = keep.tile([P, E * C], F32, name="gate_sb")
+        nc.sync.dma_start(out=gate_sb[:], in_=gate[0:P, :])
+        load_w(2)
+        load_w(3)
+
+        win = []
+        for h in range(2):
+            window = keep.tile([P, T], F32, name=f"win{h}")
+            win.append(window)
+        for e in range(E):
+            s, cols, slots = e // 2, slice((e % 2) * C, (e % 2 + 1) * C), slice(e * C, (e + 1) * C)
+            acc = []
+            for h in range(2):
+                bank = psum.tile([P, C], F32, name=f"acc{e}{h}")
+                acc.append(bank)
+            for a in range(PASSES):
+                g, k = a // 4, 4 * (a % 4)
+                for h in range(2):
+                    rows = slice(h * P, (h + 1) * P)
+                    nc.tensor.matmul_mx(
+                        out=acc[h][:],
+                        lhsT=wt[e][:, a, rows].bitcast(FP8X4),
+                        lhsT_scale=wsc[:, e * PASSES + a, rows],
+                        rhs=gw[a, s][:, cols].bitcast(FP8X4),
+                        rhs_scale=gs[g, s][k:P, cols],
+                        start=(a == 0),
+                        stop=(a == PASSES - 1),
+                    )
+            for h in range(2):
+                r = keep.tile([P, C], F32, name=f"r{e}{h}")
+                sq = keep.tile([P, C], F32, name=f"sq{e}{h}")
+                nc.scalar.activation(r[:], acc[h][:], RELU, bias=bias[:, h, e:e + 1])
+                nc.scalar.activation(sq[:], r[:], SQUARE)
+                nc.vector.tensor_tensor(win[h][:].indirect(offsets[:, e * (C // 16):(e + 1) * (C // 16)]), sq[:], gate_sb[:, slots], MULT)
+        for h in range(2):
+            nc.sync.dma_start(out=out[h * P:(h + 1) * P, :], in_=win[h][:])

@@ -19,65 +19,46 @@ RELU = mybir.ActivationFunctionType.Relu
 SQUARE = mybir.ActivationFunctionType.Square
 MULT = mybir.AluOpType.mult
 
-H = 512
-WHOLE = [(0, 1024)]
-WHOLE = [(0, 1024)]
-WHOLE = [(0, 1024)]
-HALVES = [(0, 512), (512, 1024)]
-LOADS = [[(0, 256), (256, 512), (512, 1024)], HALVES, WHOLE, WHOLE, WHOLE, [(0, 512), (512, 768), (768, 1024)]]
-MIDS = [[(0, 512)], [(512, 928)]]
-MIDV = [[], [(928, 1024)]]
-SCALAR_PART = [[[(0, 256)], [(512, 704)]], [[(0, 512)], [(512, 832)]], MIDS, MIDS, MIDS, [[(0, 512)], [(512, 768), (768, 864)]]]
-VECTOR_PART = [[[(256, 512)], [(704, 1024)]], [[], [(832, 1024)]], MIDV, MIDV, MIDV, [[], [(864, 1024)]]]
-QUANT = [512, 512, 512, 512, 512, 256]
+WINDOW = 1408
+RUN = 2
+LOADS = [[[0, 1024]], [[0, 512], [512, 1024]], [[0, 512], [512, 1024]], [[0, 512], [512, 1024]], [[0, 512], [512, 1024]], [[0, 512], [512, 768], [768, 1024]]]
+SHARES = [[["v", 512, 1024], ["s", 0, 384], ["v", 384, 512]], [["s", 0, 512], ["s", 512, 960], ["v", 960, 1024]], [["s", 0, 512], ["s", 512, 960], ["v", 960, 1024]], [["s", 0, 512], ["s", 512, 960], ["v", 960, 1024]], [["s", 0, 512], ["s", 512, 960], ["v", 960, 1024]], [["s", 0, 512], ["s", 512, 768], ["s", 768, 896], ["v", 896, 1024]]]
+QUANT = [[[0, 512], [512, 1024]], [[0, 512], [512, 1024]], [[0, 512], [512, 1024]], [[0, 512], [512, 1024]], [[0, 512], [512, 1024]], [[0, 512], [512, 768], [768, 1024]]]
+GROUP = [0, 0, 1, 1, 1, 1]
+PLANE = [0, 4, 0, 4, 8, 12]
+GATHERS = [[[0, 1024]], [[0, 1024]], [[0, 1024]], [[0, 1024]], [[0, 1024]], [[0, 256], [256, 1024]]]
+SCATTERS = [[[0, 1], [1, 2], [2, 3], [3, 4]], [[0, 2], [2, 4]]]
 
 
 def tile_routed_moe_kernel(tc, xT, w_words, w_scales, b, gate, offs, out):
     nc = tc.nc
     xv = xT.rearrange("(a p t) n -> a p t n", p=P, t=4)
+    copy_on = {"s": nc.scalar.copy, "v": nc.vector.tensor_copy, "g": nc.gpsimd.tensor_copy}
 
     with ExitStack() as ctx:
         keep = ctx.enter_context(tc.tile_pool(name="keep", bufs=1))
-        rawp = ctx.enter_context(tc.tile_pool(name="rawp", bufs=4))
-        grpp = ctx.enter_context(tc.tile_pool(name="grpp", bufs=4))
+        rawp = ctx.enter_context(tc.tile_pool(name="rawp", bufs=1))
+        grpp = ctx.enter_context(tc.tile_pool(name="grpp", bufs=3))
         psum = ctx.enter_context(tc.psum_pool(name="psum", bufs=1))
 
         offsets = keep.tile([P, E * C // 16], U16, name="offsets")
-        bias = keep.tile([P, 2, E], F32, name="bias")
-        nc.scalar.dma_start(out=bias[:], in_=b.rearrange("(h p) e -> p h e", p=P))
 
         qs = []
         for g in range(2):
-            plane = keep.tile([P, T], U8, name=f"qs{g}", align_bytes=64)
-            nc.vector.memset(plane[:].bitcast(I32), 0)
+            plane = keep.tile([P, WINDOW], U8, name=f"qs{g}", align_bytes=64)
+            nc.vector.memset(plane[:, 0:T].bitcast(I32), 0)
             qs.append(plane)
         wsc = keep.tile([P, E * PASSES, N], U8, name="wsc", align_bytes=64)
         nc.vector.memset(wsc[:].bitcast(I32), 0)
 
-        gw = {}
-        gs = {}
+        gw = []
+        gs = []
+        for g in range(2):
+            gathered = keep.tile([P, T], U8, name=f"gs{g}", align_bytes=64)
+            gs.append(gathered)
 
-        def gather_bytes(g, s):
-            t = keep.tile([P, H], U8, name=f"gs{g}{s}", align_bytes=64)
-            nc.vector.tensor_copy(t[:], qs[g][:].indirect(offsets[:, s * (H // 16):(s + 1) * (H // 16)]))
-            gs[g, s] = t
-
-        def gather_words(a, s, words):
-            t = keep.tile([P, H], U32, name=f"gw{a}{s}", align_bytes=64)
-            nc.vector.tensor_copy(t[:], words[:].indirect(offsets[:, s * (H // 16):(s + 1) * (H // 16)]))
-            gw[a, s] = t
-
-        wv = w_scales.rearrange("e a q n -> q (e a) n")
-        wt = {}
-
-        def load_scales():
-            for q in range(4):
-                nc.sync.dma_start(out=wsc[32 * q:32 * q + 4].bitcast(I32), in_=wv[4 * q:4 * q + 4].bitcast(I32))
-
-        def load_w(e):
-            w = keep.tile([P, PASSES, N], U32, name=f"w{e}", align_bytes=64)
-            nc.sync.dma_start(out=w[:].bitcast(I32), in_=w_words[e].rearrange("a p n r -> p a (n r)").bitcast(I32))
-            wt[e] = w
+        def slots_of(lo, hi):
+            return offsets[:, lo // 16:hi // 16]
 
         def find(pieces, lo, hi):
             for plo, phi, tile in pieces:
@@ -85,75 +66,77 @@ def tile_routed_moe_kernel(tc, xT, w_words, w_scales, b, gate, offs, out):
                     return tile[:, :, lo - plo:hi - plo]
 
         for a in range(PASSES):
-            words = keep.tile([P, T], U32, name=f"qw{a}", align_bytes=64)
-            g, k = a // 4, 4 * (a % 4)
-            if a == 5:
-                load_scales()
+            words = grpp.tile([P, WINDOW], U32, name="words", align_bytes=64)
+            gathered = keep.tile([P, T], U32, name=f"gw{a}", align_bytes=64)
+            gw.append(gathered)
+            g, k = GROUP[a], PLANE[a]
             pieces = []
             for lo, hi in LOADS[a]:
-                raw = rawp.tile([P, 4, hi - lo], F32, name=f"raw{hi - lo}", bufs={1024: 3, 512: 4, 256: 4}[hi - lo], align_bytes=64)
+                raw = rawp.tile([P, 4, hi - lo], F32, name=f"raw{hi - lo}", bufs={1024: 1, 512: 6, 256: 2}[hi - lo], align_bytes=64)
                 nc.sync.dma_start(out=raw[:], in_=xv[a, :, :, lo:hi])
                 pieces.append((lo, hi, raw))
                 if a == 0 and lo == 0:
                     nc.sync.dma_start(offsets[:], offs)
-            halves = []
-            for s in range(2):
-                grouped = grpp.tile([P, H, 4], BF16, name="grouped", align_bytes=64)
-                halves.append(grouped)
-                for engine, parts in ((nc.scalar.copy, SCALAR_PART[a][s]), (nc.vector.tensor_copy, VECTOR_PART[a][s])):
-                    for lo, hi in parts:
-                        engine(
-                            grouped[:, lo - s * H:hi - s * H, :].rearrange("p (c i) t -> p c t i", i=4),
-                            find(pieces, lo, hi).rearrange("p t (c i) -> p c t i", i=4),
-                        )
-            for s in range(2):
-                for lo in range(0, H, QUANT[a]):
-                    cols = slice(s * H + lo, s * H + lo + QUANT[a])
-                    nc.vector.quantize_mx(
-                        out=words[:, cols].bitcast(FP8X4),
-                        scales=qs[g][k:P, cols],
-                        in_=halves[s][:, lo:lo + QUANT[a], :].rearrange("p n t -> p (n t)"),
-                    )
-            for s in range(2):
-                if a in (3, 5):
-                    gather_bytes(g, s)
-                gather_words(a, s, words)
+            grouped = grpp.tile([P, T, 4], BF16, name="grouped", align_bytes=64)
+            for engine, lo, hi in SHARES[a]:
+                copy_on[engine](
+                    grouped[:, lo:hi, :].rearrange("p (c i) t -> p c t i", i=RUN),
+                    find(pieces, lo, hi).rearrange("p t (c i) -> p c t i", i=RUN),
+                )
+            for lo, hi in QUANT[a]:
+                nc.vector.quantize_mx(
+                    out=words[:, lo:hi].bitcast(FP8X4),
+                    scales=qs[g][k:P, lo:hi],
+                    in_=grouped[:, lo:hi, :].rearrange("p n t -> p (n t)"),
+                )
+            for lo, hi in GATHERS[a]:
+                if a + 1 == PASSES or GROUP[a + 1] != g:
+                    nc.vector.tensor_copy(gs[g][:, lo:hi], qs[g][:].indirect(slots_of(lo, hi)))
+                nc.vector.tensor_copy(gathered[:, lo:hi], words[:].indirect(slots_of(lo, hi)))
 
-        load_w(0)
-        load_w(1)
+        wv = w_scales.rearrange("e a q n -> q (e a) n")
+        for q in range(4):
+            nc.sync.dma_start(out=wsc[32 * q:32 * q + 4].bitcast(I32), in_=wv[4 * q:4 * q + 4].bitcast(I32))
+
+        wt = {}
+
+        def load_w(e, h):
+            w = keep.tile([P, PASSES, P], U32, name=f"w{e}{h}", align_bytes=64)
+            nc.sync.dma_start(out=w[:].bitcast(I32), in_=w_words[e].rearrange("a p n r -> p a (n r)")[:, :, h * 4 * P:(h + 1) * 4 * P].bitcast(I32))
+            wt[e, h] = w
+
+        bias = keep.tile([P, 2, E], F32, name="bias")
         gate_sb = keep.tile([P, E * C], F32, name="gate_sb")
-        nc.sync.dma_start(out=gate_sb[:], in_=gate[0:P, :])
-        load_w(2)
-        load_w(3)
-
-        win = []
-        for h in range(2):
-            window = keep.tile([P, T], F32, name=f"win{h}")
-            win.append(window)
+        load_w(0, 0)
+        nc.sync.dma_start(out=bias[:], in_=b.rearrange("(h p) e -> p h e", p=P))
+        nc.sync.dma_start(out=gate_sb[:, 0:2 * C], in_=gate[0:P, 0:2 * C])
+        load_w(1, 0)
+        load_w(2, 0)
+        nc.sync.dma_start(out=gate_sb[:, 2 * C:4 * C], in_=gate[0:P, 2 * C:4 * C])
+        load_w(3, 0)
         for e in range(E):
-            s, cols, slots = e // 2, slice((e % 2) * C, (e % 2 + 1) * C), slice(e * C, (e + 1) * C)
-            acc = []
-            for h in range(2):
-                bank = psum.tile([P, C], F32, name=f"acc{e}{h}")
-                acc.append(bank)
-            for a in range(PASSES):
-                g, k = a // 4, 4 * (a % 4)
-                for h in range(2):
-                    rows = slice(h * P, (h + 1) * P)
+            load_w(e, 1)
+
+        for h in range(2):
+            rows = slice(h * P, (h + 1) * P)
+            window = keep.tile([P, T], F32, name=f"win{h}")
+            sq = keep.tile([P, E * C], F32, name=f"sq{h}")
+            for e in range(E):
+                slots = slice(e * C, (e + 1) * C)
+                acc = psum.tile([P, C], F32, name=f"acc{e}{h}")
+                for a in range(PASSES):
                     nc.tensor.matmul_mx(
-                        out=acc[h][:],
-                        lhsT=wt[e][:, a, rows].bitcast(FP8X4),
+                        out=acc[:],
+                        lhsT=wt[e, h][:, a, :].bitcast(FP8X4),
                         lhsT_scale=wsc[:, e * PASSES + a, rows],
-                        rhs=gw[a, s][:, cols].bitcast(FP8X4),
-                        rhs_scale=gs[g, s][k:P, cols],
+                        rhs=gw[a][:, slots].bitcast(FP8X4),
+                        rhs_scale=gs[GROUP[a]][PLANE[a]:P, slots],
                         start=(a == 0),
                         stop=(a == PASSES - 1),
                     )
-            for h in range(2):
-                r = keep.tile([P, C], F32, name=f"r{e}{h}")
-                sq = keep.tile([P, C], F32, name=f"sq{e}{h}")
-                nc.scalar.activation(r[:], acc[h][:], RELU, bias=bias[:, h, e:e + 1])
-                nc.scalar.activation(sq[:], r[:], SQUARE)
-                nc.vector.tensor_tensor(win[h][:].indirect(offsets[:, e * (C // 16):(e + 1) * (C // 16)]), sq[:], gate_sb[:, slots], MULT)
-        for h in range(2):
-            nc.sync.dma_start(out=out[h * P:(h + 1) * P, :], in_=win[h][:])
+                r = grpp.tile([P, C], F32, name="r")
+                nc.scalar.activation(r[:], acc[:], RELU, bias=bias[:, h, e:e + 1])
+                nc.scalar.activation(sq[:, slots], r[:], SQUARE)
+            for lo, hi in SCATTERS[h]:
+                nc.vector.tensor_tensor(window[:].indirect(slots_of(lo * C, hi * C)), sq[:, lo * C:hi * C], gate_sb[:, lo * C:hi * C], MULT)
+            nc.sync.dma_start(out=out[rows, :], in_=window[:])

@@ -20,14 +20,13 @@ SQUARE = mybir.ActivationFunctionType.Square
 MULT = mybir.AluOpType.mult
 
 WINDOW = 1408
-RUN = 2
-LOADS = [[[0, 1024]], [[0, 512], [512, 1024]], [[0, 512], [512, 1024]], [[0, 512], [512, 1024]], [[0, 512], [512, 1024]], [[0, 512], [512, 768], [768, 1024]]]
-SHARES = [[["v", 512, 1024], ["s", 0, 384], ["v", 384, 512]], [["s", 0, 512], ["s", 512, 960], ["v", 960, 1024]], [["s", 0, 512], ["s", 512, 960], ["v", 960, 1024]], [["s", 0, 512], ["s", 512, 960], ["v", 960, 1024]], [["s", 0, 512], ["s", 512, 960], ["v", 960, 1024]], [["s", 0, 512], ["s", 512, 768], ["s", 768, 896], ["v", 896, 1024]]]
-QUANT = [[[0, 512], [512, 1024]], [[0, 512], [512, 1024]], [[0, 512], [512, 1024]], [[0, 512], [512, 1024]], [[0, 512], [512, 1024]], [[0, 512], [512, 768], [768, 1024]]]
+RUN = 4
+LOADS = [[[0, 1024]], [[0, 1024]], [[0, 1024]], [[0, 1024]], [[0, 1024]], [[0, 1024]]]
+SHARES = [[["s", 0, 512], ["v", 512, 1024]], [["s", 0, 512], ["v", 640, 1024], ["s", 512, 640]], [["s", 0, 512], ["v", 896, 1024], ["s", 512, 896]], [["s", 0, 512], ["v", 896, 1024], ["s", 512, 896]], [["s", 0, 512], ["v", 896, 1024], ["s", 512, 896]], [["s", 0, 512], ["v", 768, 1024], ["s", 512, 768]]]
+QUANT = [[[0, 512], [512, 1024]], [[0, 512], [512, 1024]], [[0, 512], [512, 1024]], [[0, 512], [512, 1024]], [[0, 512], [512, 1024]], [[0, 512], [512, 1024]]]
 GROUP = [0, 0, 1, 1, 1, 1]
 PLANE = [0, 4, 0, 4, 8, 12]
 GATHERS = [[[0, 1024]], [[0, 1024]], [[0, 1024]], [[0, 1024]], [[0, 1024]], [[0, 256], [256, 1024]]]
-SCATTERS = [[[0, 1], [1, 2], [2, 3], [3, 4]], [[0, 2], [2, 4]]]
 
 
 def tile_routed_moe_kernel(tc, xT, w_words, w_scales, b, gate, offs, out):
@@ -72,7 +71,7 @@ def tile_routed_moe_kernel(tc, xT, w_words, w_scales, b, gate, offs, out):
             g, k = GROUP[a], PLANE[a]
             pieces = []
             for lo, hi in LOADS[a]:
-                raw = rawp.tile([P, 4, hi - lo], F32, name=f"raw{hi - lo}", bufs={1024: 1, 512: 6, 256: 2}[hi - lo], align_bytes=64)
+                raw = rawp.tile([P, 4, hi - lo], F32, name=f"raw{hi - lo}", bufs={1024: 4}[hi - lo], align_bytes=64)
                 nc.sync.dma_start(out=raw[:], in_=xv[a, :, :, lo:hi])
                 pieces.append((lo, hi, raw))
                 if a == 0 and lo == 0:
@@ -98,45 +97,36 @@ def tile_routed_moe_kernel(tc, xT, w_words, w_scales, b, gate, offs, out):
         for q in range(4):
             nc.sync.dma_start(out=wsc[32 * q:32 * q + 4].bitcast(I32), in_=wv[4 * q:4 * q + 4].bitcast(I32))
 
-        wt = {}
-
-        def load_w(e, h):
-            w = keep.tile([P, PASSES, P], U32, name=f"w{e}{h}", align_bytes=64)
-            nc.sync.dma_start(out=w[:].bitcast(I32), in_=w_words[e].rearrange("a p n r -> p a (n r)")[:, :, h * 4 * P:(h + 1) * 4 * P].bitcast(I32))
-            wt[e, h] = w
-
+        wt = []
         bias = keep.tile([P, 2, E], F32, name="bias")
         gate_sb = keep.tile([P, E * C], F32, name="gate_sb")
-        load_w(0, 0)
-        nc.sync.dma_start(out=bias[:], in_=b.rearrange("(h p) e -> p h e", p=P))
-        nc.sync.dma_start(out=gate_sb[:, 0:2 * C], in_=gate[0:P, 0:2 * C])
-        load_w(1, 0)
-        load_w(2, 0)
-        nc.sync.dma_start(out=gate_sb[:, 2 * C:4 * C], in_=gate[0:P, 2 * C:4 * C])
-        load_w(3, 0)
         for e in range(E):
-            load_w(e, 1)
+            w = keep.tile([P, PASSES, N], U32, name=f"w{e}", align_bytes=64)
+            nc.sync.dma_start(out=w[:].bitcast(I32), in_=w_words[e].rearrange("a p n r -> p a (n r)").bitcast(I32))
+            wt.append(w)
+            if e == 0:
+                nc.sync.dma_start(out=bias[:], in_=b.rearrange("(h p) e -> p h e", p=P))
+                nc.sync.dma_start(out=gate_sb[:], in_=gate[0:P, :])
 
-        for h in range(2):
+        windows = [keep.tile([P, T], F32, name=f"win{h}") for h in range(2)]
+        for e, h in sorted(((e, h) for e in range(E) for h in range(2)), key=lambda eh: 2 * eh[0] + 3 * eh[1]):
             rows = slice(h * P, (h + 1) * P)
-            window = keep.tile([P, T], F32, name=f"win{h}")
-            sq = keep.tile([P, E * C], F32, name=f"sq{h}")
-            for e in range(E):
-                slots = slice(e * C, (e + 1) * C)
-                acc = psum.tile([P, C], F32, name=f"acc{e}{h}")
-                for a in range(PASSES):
-                    nc.tensor.matmul_mx(
-                        out=acc[:],
-                        lhsT=wt[e, h][:, a, :].bitcast(FP8X4),
-                        lhsT_scale=wsc[:, e * PASSES + a, rows],
-                        rhs=gw[a][:, slots].bitcast(FP8X4),
-                        rhs_scale=gs[GROUP[a]][PLANE[a]:P, slots],
-                        start=(a == 0),
-                        stop=(a == PASSES - 1),
-                    )
-                r = grpp.tile([P, C], F32, name="r")
-                nc.scalar.activation(r[:], acc[:], RELU, bias=bias[:, h, e:e + 1])
-                nc.scalar.activation(sq[:, slots], r[:], SQUARE)
-            for lo, hi in SCATTERS[h]:
-                nc.vector.tensor_tensor(window[:].indirect(slots_of(lo * C, hi * C)), sq[:, lo * C:hi * C], gate_sb[:, lo * C:hi * C], MULT)
-            nc.sync.dma_start(out=out[rows, :], in_=window[:])
+            slots = slice(e * C, (e + 1) * C)
+            acc = psum.tile([P, C], F32, name=f"acc{e}{h}")
+            for a in range(PASSES):
+                nc.tensor.matmul_mx(
+                    out=acc[:],
+                    lhsT=wt[e][:, a, rows].bitcast(FP8X4),
+                    lhsT_scale=wsc[:, e * PASSES + a, rows],
+                    rhs=gw[a][:, slots].bitcast(FP8X4),
+                    rhs_scale=gs[GROUP[a]][PLANE[a]:P, slots],
+                    start=(a == 0),
+                    stop=(a == PASSES - 1),
+                )
+            r = grpp.tile([P, C], F32, name="r")
+            sq = keep.tile([P, C], F32, name=f"sq{e}{h}")
+            nc.scalar.activation(r[:], acc[:], RELU, bias=bias[:, h, e:e + 1])
+            nc.scalar.activation(sq[:], r[:], SQUARE)
+            nc.vector.tensor_tensor(windows[h][:].indirect(slots_of(e * C, (e + 1) * C)), sq[:], gate_sb[:, slots], MULT)
+            if e == E - 1:
+                nc.sync.dma_start(out=out[rows, :], in_=windows[h][:])

@@ -109,19 +109,20 @@ def tile_routed_moe_kernel(tc, xT, w_words, w_scales, b, gate, offs, out):
                 nc.sync.dma_start(out=gate_sb[:], in_=gate[0:P, :])
 
         windows = [keep.tile([P, T], F32, name=f"win{h}") for h in range(2)]
-        for e, h in sorted(((e, h) for e in range(E) for h in range(2)), key=lambda eh: 2 * eh[0] + 3 * eh[1]):
+        order = [(e, h) for e in range(E - 2) for h in range(2)] + [(e, h) for h in range(2) for e in range(E - 2, E)]
+        for e, h in order:
             rows = slice(h * P, (h + 1) * P)
             slots = slice(e * C, (e + 1) * C)
             acc = psum.tile([P, C], F32, name=f"acc{e}{h}")
-            for a in range(PASSES):
+            for a in reversed(range(PASSES)):
                 nc.tensor.matmul_mx(
                     out=acc[:],
                     lhsT=wt[e][:, a, rows].bitcast(FP8X4),
                     lhsT_scale=wsc[:, e * PASSES + a, rows],
                     rhs=gw[a][:, slots].bitcast(FP8X4),
                     rhs_scale=gs[GROUP[a]][PLANE[a]:P, slots],
-                    start=(a == 0),
-                    stop=(a == PASSES - 1),
+                    start=(a == PASSES - 1),
+                    stop=(a == 0),
                 )
             r = grpp.tile([P, C], F32, name="r")
             sq = keep.tile([P, C], F32, name=f"sq{e}{h}")

@@ -5,8 +5,10 @@ import concourse.mybir as mybir
 K, T, E, C, N = 3072, 1024, 4, 256, 256
 P = 128
 PASSES = K // 512
-FLOPS = 2 * K * N * E * C
-BYTES = 4 * K * T + E * K * N + E * K * N // 32 + 4 * N * E + 4 * E * C + 2 * P * (E * C // 16) + 4 * N * T
+SLOTS = E * C
+BLOCKS = N // P
+FLOPS = 2 * K * N * SLOTS
+BYTES = 4 * K * T + E * K * N + E * K * N // 32 + 4 * N * E + 4 * SLOTS + 2 * P * (SLOTS // 16) + 4 * N * T
 
 F32 = mybir.dt.float32
 BF16 = mybir.dt.bfloat16
@@ -19,115 +21,125 @@ RELU = mybir.ActivationFunctionType.Relu
 SQUARE = mybir.ActivationFunctionType.Square
 MULT = mybir.AluOpType.mult
 
+HALF = T // 2
+
 WINDOW = 1408
-RUN = 4
-LOADS = [[[0, 1024]], [[0, 1024]], [[0, 1024]], [[0, 1024]], [[0, 1024]], [[0, 1024]]]
-SHARES = [[["s", 0, 512], ["v", 512, 1024]], [["s", 0, 512], ["v", 640, 1024], ["s", 512, 640]], [["s", 0, 512], ["v", 896, 1024], ["s", 512, 896]], [["s", 0, 512], ["v", 896, 1024], ["s", 512, 896]], [["s", 0, 512], ["v", 896, 1024], ["s", 512, 896]], [["s", 0, 512], ["v", 768, 1024], ["s", 512, 768]]]
-QUANT = [[[0, 512], [512, 1024]], [[0, 512], [512, 1024]], [[0, 512], [512, 1024]], [[0, 512], [512, 1024]], [[0, 512], [512, 1024]], [[0, 512], [512, 1024]]]
-GROUP = [0, 0, 1, 1, 1, 1]
-PLANE = [0, 4, 0, 4, 8, 12]
-GATHERS = [[[0, 1024]], [[0, 1024]], [[0, 1024]], [[0, 1024]], [[0, 1024]], [[0, 256], [256, 1024]]]
+
+PLANES_FROM = (0, 2)
+
+VECTOR_SHARE = (512, 448, 0, 128, 256, 256)
 
 
 def tile_routed_moe_kernel(tc, xT, w_words, w_scales, b, gate, offs, out):
     nc = tc.nc
-    xv = xT.rearrange("(a p t) n -> a p t n", p=P, t=4)
-    copy_on = {"s": nc.scalar.copy, "v": nc.vector.tensor_copy, "g": nc.gpsimd.tensor_copy}
+    x_passes = xT.rearrange("(a p t) n -> a p t n", p=P, t=4)
 
     with ExitStack() as ctx:
         keep = ctx.enter_context(tc.tile_pool(name="keep", bufs=1))
-        rawp = ctx.enter_context(tc.tile_pool(name="rawp", bufs=1))
-        grpp = ctx.enter_context(tc.tile_pool(name="grpp", bufs=3))
+        loads = ctx.enter_context(tc.tile_pool(name="loads", bufs=4))
+        ring = ctx.enter_context(tc.tile_pool(name="ring", bufs=3))
         psum = ctx.enter_context(tc.psum_pool(name="psum", bufs=1))
 
-        offsets = keep.tile([P, E * C // 16], U16, name="offsets")
+        offsets = keep.tile([P, SLOTS // 16], U16, name="offsets")
 
-        qs = []
-        for g in range(2):
-            plane = keep.tile([P, WINDOW], U8, name=f"qs{g}", align_bytes=64)
-            nc.vector.memset(plane[:, 0:T].bitcast(I32), 0)
-            qs.append(plane)
-        wsc = keep.tile([P, E * PASSES, N], U8, name="wsc", align_bytes=64)
-        nc.vector.memset(wsc[:].bitcast(I32), 0)
-
-        gw = []
-        gs = []
-        for g in range(2):
-            gathered = keep.tile([P, T], U8, name=f"gs{g}", align_bytes=64)
-            gs.append(gathered)
-
-        def slots_of(lo, hi):
+        def entries(lo, hi):
             return offsets[:, lo // 16:hi // 16]
 
-        def find(pieces, lo, hi):
-            for plo, phi, tile in pieces:
-                if plo <= lo and hi <= phi:
-                    return tile[:, :, lo - plo:hi - plo]
+        token_scales = []
+        for g in range(len(PLANES_FROM)):
+            planes = keep.tile([P, WINDOW], U8, name=f"token_scales{g}", align_bytes=64)
+            nc.vector.memset(planes[:, 0:T].bitcast(I32), 0)
+            token_scales.append(planes)
+        weight_scales = keep.tile([P, E * PASSES, N], U8, name="weight_scales", align_bytes=64)
+        nc.vector.memset(weight_scales[:].bitcast(I32), 0)
+
+        slot_scales = [keep.tile([P, SLOTS], U8, name=f"slot_scales{g}", align_bytes=64) for g in range(len(PLANES_FROM))]
+        slot_words = []
+
+        def plane_of(a):
+            g = len([start for start in PLANES_FROM if start <= a]) - 1
+            return g, 4 * (a - PLANES_FROM[g])
+
+        def interleave(copy, grouped, raw, lo, hi):
+            copy(
+                grouped[:, lo:hi, :].rearrange("p (c i) t -> p c t i", i=4),
+                raw[:, :, lo:hi].rearrange("p t (c i) -> p c t i", i=4),
+            )
 
         for a in range(PASSES):
-            words = grpp.tile([P, WINDOW], U32, name="words", align_bytes=64)
-            gathered = keep.tile([P, T], U32, name=f"gw{a}", align_bytes=64)
-            gw.append(gathered)
-            g, k = GROUP[a], PLANE[a]
-            pieces = []
-            for lo, hi in LOADS[a]:
-                raw = rawp.tile([P, 4, hi - lo], F32, name=f"raw{hi - lo}", bufs={1024: 4}[hi - lo], align_bytes=64)
-                nc.sync.dma_start(out=raw[:], in_=xv[a, :, :, lo:hi])
-                pieces.append((lo, hi, raw))
-                if a == 0 and lo == 0:
-                    nc.sync.dma_start(offsets[:], offs)
-            grouped = grpp.tile([P, T, 4], BF16, name="grouped", align_bytes=64)
-            for engine, lo, hi in SHARES[a]:
-                copy_on[engine](
-                    grouped[:, lo:hi, :].rearrange("p (c i) t -> p c t i", i=RUN),
-                    find(pieces, lo, hi).rearrange("p t (c i) -> p c t i", i=RUN),
-                )
-            for lo, hi in QUANT[a]:
+            token_words = ring.tile([P, WINDOW], U32, name="token_words", align_bytes=64)
+            gathered = keep.tile([P, SLOTS], U32, name=f"slot_words{a}", align_bytes=64)
+            slot_words.append(gathered)
+            g, first = plane_of(a)
+
+            raw = loads.tile([P, 4, T], F32, name="raw", align_bytes=64)
+            nc.sync.dma_start(out=raw[:], in_=x_passes[a])
+            if a == 0:
+                nc.sync.dma_start(offsets[:], offs)
+
+            grouped = ring.tile([P, T, 4], BF16, name="grouped", align_bytes=64)
+            split = T - VECTOR_SHARE[a]
+            interleave(nc.scalar.copy, grouped, raw, 0, HALF)
+            if split < T:
+                interleave(nc.vector.tensor_copy, grouped, raw, split, T)
+            if HALF < split:
+                interleave(nc.scalar.copy, grouped, raw, HALF, split)
+
+            for lo in range(0, T, HALF):
                 nc.vector.quantize_mx(
-                    out=words[:, lo:hi].bitcast(FP8X4),
-                    scales=qs[g][k:P, lo:hi],
-                    in_=grouped[:, lo:hi, :].rearrange("p n t -> p (n t)"),
+                    out=token_words[:, lo:lo + HALF].bitcast(FP8X4),
+                    scales=token_scales[g][first:P, lo:lo + HALF],
+                    in_=grouped[:, lo:lo + HALF, :].rearrange("p n t -> p (n t)"),
                 )
-            for lo, hi in GATHERS[a]:
-                if a + 1 == PASSES or GROUP[a + 1] != g:
-                    nc.vector.tensor_copy(gs[g][:, lo:hi], qs[g][:].indirect(slots_of(lo, hi)))
-                nc.vector.tensor_copy(gathered[:, lo:hi], words[:].indirect(slots_of(lo, hi)))
 
-        wv = w_scales.rearrange("e a q n -> q (e a) n")
-        for q in range(4):
-            nc.sync.dma_start(out=wsc[32 * q:32 * q + 4].bitcast(I32), in_=wv[4 * q:4 * q + 4].bitcast(I32))
+            last_pass = a == PASSES - 1
+            planes_done = last_pass or a + 1 in PLANES_FROM
+            for lo, hi in ((0, C), (C, SLOTS)) if last_pass else ((0, SLOTS),):
+                if planes_done:
+                    nc.vector.tensor_copy(slot_scales[g][:, lo:hi], token_scales[g][:].indirect(entries(lo, hi)))
+                nc.vector.tensor_copy(gathered[:, lo:hi], token_words[:].indirect(entries(lo, hi)))
 
-        wt = []
-        bias = keep.tile([P, 2, E], F32, name="bias")
-        gate_sb = keep.tile([P, E * C], F32, name="gate_sb")
+        scale_rows = w_scales.rearrange("e a q n -> q (e a) n")
+        for quadrant in range(4):
+            nc.sync.dma_start(
+                out=weight_scales[32 * quadrant:32 * quadrant + 4].bitcast(I32),
+                in_=scale_rows[4 * quadrant:4 * quadrant + 4].bitcast(I32),
+            )
+
+        weights = []
+        bias = keep.tile([P, BLOCKS, E], F32, name="bias")
+        gate_rows = keep.tile([P, SLOTS], F32, name="gate_rows")
         for e in range(E):
-            w = keep.tile([P, PASSES, N], U32, name=f"w{e}", align_bytes=64)
-            nc.sync.dma_start(out=w[:].bitcast(I32), in_=w_words[e].rearrange("a p n r -> p a (n r)").bitcast(I32))
-            wt.append(w)
+            codes = keep.tile([P, PASSES, N], U32, name=f"weights{e}", align_bytes=64)
+            nc.sync.dma_start(out=codes[:].bitcast(I32), in_=w_words[e].rearrange("a p n r -> p a (n r)").bitcast(I32))
+            weights.append(codes)
             if e == 0:
                 nc.sync.dma_start(out=bias[:], in_=b.rearrange("(h p) e -> p h e", p=P))
-                nc.sync.dma_start(out=gate_sb[:], in_=gate[0:P, :])
+                nc.sync.dma_start(out=gate_rows[:], in_=gate[0:P, :])
 
-        windows = [keep.tile([P, T], F32, name=f"win{h}") for h in range(2)]
-        order = [(e, h) for e in range(E - 2) for h in range(2)] + [(e, h) for h in range(2) for e in range(E - 2, E)]
-        for e, h in order:
-            rows = slice(h * P, (h + 1) * P)
+        results = [keep.tile([P, T], F32, name=f"results{h}") for h in range(BLOCKS)]
+        squares = [keep.tile([P, SLOTS], F32, name=f"squares{h}") for h in range(BLOCKS)]
+        for e in range(E):
             slots = slice(e * C, (e + 1) * C)
-            acc = psum.tile([P, C], F32, name=f"acc{e}{h}")
-            for a in reversed(range(PASSES)):
-                nc.tensor.matmul_mx(
-                    out=acc[:],
-                    lhsT=wt[e][:, a, rows].bitcast(FP8X4),
-                    lhsT_scale=wsc[:, e * PASSES + a, rows],
-                    rhs=gw[a][:, slots].bitcast(FP8X4),
-                    rhs_scale=gs[GROUP[a]][PLANE[a]:P, slots],
-                    start=(a == PASSES - 1),
-                    stop=(a == 0),
+            for h in range(BLOCKS):
+                features = slice(h * P, (h + 1) * P)
+                sums = psum.tile([P, C], F32, name=f"sums{e}{h}")
+                for a in reversed(range(PASSES)):
+                    g, first = plane_of(a)
+                    nc.tensor.matmul_mx(
+                        out=sums[:],
+                        lhsT=weights[e][:, a, features].bitcast(FP8X4),
+                        lhsT_scale=weight_scales[:, e * PASSES + a, features],
+                        rhs=slot_words[a][:, slots].bitcast(FP8X4),
+                        rhs_scale=slot_scales[g][first:P, slots],
+                        start=(a == PASSES - 1),
+                        stop=(a == 0),
+                    )
+                positive = ring.tile([P, C], F32, name="positive")
+                nc.scalar.activation(positive[:], sums[:], RELU, bias=bias[:, h, e:e + 1])
+                nc.scalar.activation(squares[h][:, slots], positive[:], SQUARE)
+                nc.vector.tensor_tensor(
+                    results[h][:].indirect(entries(slots.start, slots.stop)), squares[h][:, slots], gate_rows[:, slots], MULT
                 )
-            r = grpp.tile([P, C], F32, name="r")
-            sq = keep.tile([P, C], F32, name=f"sq{e}{h}")
-            nc.scalar.activation(r[:], acc[:], RELU, bias=bias[:, h, e:e + 1])
-            nc.scalar.activation(sq[:], r[:], SQUARE)
-            nc.vector.tensor_tensor(windows[h][:].indirect(slots_of(e * C, (e + 1) * C)), sq[:], gate_sb[:, slots], MULT)
-            if e == E - 1:
-                nc.sync.dma_start(out=out[rows, :], in_=windows[h][:])
+                if e == E - 1:
+                    nc.sync.dma_start(out=out[features, :], in_=results[h][:])

@@ -27,7 +27,7 @@ WINDOW = 1408
 
 PLANES_FROM = (0, 2)
 
-VECTOR_SHARE = (512, 448, 0, 128, 256, 256)
+VECTOR_SHARE = (512, 384, 0, 128, 128, 192)
 
 
 def tile_routed_moe_kernel(tc, xT, w_words, w_scales, b, gate, offs, out):

@@ -27,7 +27,7 @@ WINDOW = 1408
 
 PLANES_FROM = (0, 2)
 
-VECTOR_SHARE = (512, 384, 0, 128, 128, 192)
+HELPER_SHARE = 384
 
 
 def tile_routed_moe_kernel(tc, xT, w_words, w_scales, b, gate, offs, out):
@@ -38,6 +38,7 @@ def tile_routed_moe_kernel(tc, xT, w_words, w_scales, b, gate, offs, out):
         keep = ctx.enter_context(tc.tile_pool(name="keep", bufs=1))
         loads = ctx.enter_context(tc.tile_pool(name="loads", bufs=4))
         ring = ctx.enter_context(tc.tile_pool(name="ring", bufs=3))
+        single = ctx.enter_context(tc.tile_pool(name="single", bufs=1))
         psum = ctx.enter_context(tc.psum_pool(name="psum", bufs=1))
 
         offsets = keep.tile([P, SLOTS // 16], U16, name="offsets")
@@ -60,11 +61,8 @@ def tile_routed_moe_kernel(tc, xT, w_words, w_scales, b, gate, offs, out):
             g = len([start for start in PLANES_FROM if start <= a]) - 1
             return g, 4 * (a - PLANES_FROM[g])
 
-        def interleave(copy, grouped, raw, lo, hi):
-            copy(
-                grouped[:, lo:hi, :].rearrange("p (c i) t -> p c t i", i=4),
-                raw[:, :, lo:hi].rearrange("p t (c i) -> p c t i", i=4),
-            )
+        def interleave(copy, grouped, raw):
+            copy(grouped.rearrange("p (c i) t -> p c t i", i=4), raw.rearrange("p t (c i) -> p c t i", i=4))
 
         for a in range(PASSES):
             token_words = ring.tile([P, WINDOW], U32, name="token_words", align_bytes=64)
@@ -77,19 +75,22 @@ def tile_routed_moe_kernel(tc, xT, w_words, w_scales, b, gate, offs, out):
             if a == 0:
                 nc.sync.dma_start(offsets[:], offs)
 
-            grouped = ring.tile([P, T, 4], BF16, name="grouped", align_bytes=64)
-            split = T - VECTOR_SHARE[a]
-            interleave(nc.scalar.copy, grouped, raw, 0, HALF)
-            if split < T:
-                interleave(nc.vector.tensor_copy, grouped, raw, split, T)
-            if HALF < split:
-                interleave(nc.scalar.copy, grouped, raw, HALF, split)
+            upper = ring.tile([P, HALF, 4], BF16, name="upper", align_bytes=64)
+            lower = single.tile([P, HALF, 4], BF16, name="lower", align_bytes=64)
+            if a == 0:
+                interleave(nc.vector.tensor_copy, upper[:], raw[:, :, HALF:T])
+                interleave(nc.scalar.copy, lower[:, 0:HELPER_SHARE, :], raw[:, :, 0:HELPER_SHARE])
+                interleave(nc.vector.tensor_copy, lower[:, HELPER_SHARE:HALF, :], raw[:, :, HELPER_SHARE:HALF])
+            else:
+                interleave(nc.scalar.copy, upper[:], raw[:, :, HALF:T])
+                nc.gpsimd.tensor_copy(lower[:, 0:HELPER_SHARE, :], raw[:, :, 0:HELPER_SHARE].rearrange("p t n -> p n t"))
+                interleave(nc.scalar.copy, lower[:, HELPER_SHARE:HALF, :], raw[:, :, HELPER_SHARE:HALF])
 
-            for lo in range(0, T, HALF):
+            for lo, grouped in ((HALF, upper), (0, lower)):
                 nc.vector.quantize_mx(
                     out=token_words[:, lo:lo + HALF].bitcast(FP8X4),
                     scales=token_scales[g][first:P, lo:lo + HALF],
-                    in_=grouped[:, lo:lo + HALF, :].rearrange("p n t -> p (n t)"),
+                    in_=grouped[:].rearrange("p n t -> p (n t)"),
                 )
 
             last_pass = a == PASSES - 1

@@ -27,7 +27,9 @@ WINDOW = 1408
 
 PLANES_FROM = (0, 2)
 
-HELPER_SHARE = 384
+VECTOR_UPPER = (512, 0, 0, 0, 0, 0)
+VECTOR_LOWER = (128, 384, 0, 0, 0, 0)
+GPSIMD_LOWER = (0, 0, 288, 288, 288, 320)
 
 
 def tile_routed_moe_kernel(tc, xT, w_words, w_scales, b, gate, offs, out):
@@ -77,26 +79,31 @@ def tile_routed_moe_kernel(tc, xT, w_words, w_scales, b, gate, offs, out):
 
             upper = ring.tile([P, HALF, 4], BF16, name="upper", align_bytes=64)
             lower = single.tile([P, HALF, 4], BF16, name="lower", align_bytes=64)
-            if a == 0:
-                interleave(nc.vector.tensor_copy, upper[:], raw[:, :, HALF:T])
-                interleave(nc.scalar.copy, lower[:, 0:HELPER_SHARE, :], raw[:, :, 0:HELPER_SHARE])
-                interleave(nc.vector.tensor_copy, lower[:, HELPER_SHARE:HALF, :], raw[:, :, HELPER_SHARE:HALF])
-            else:
-                interleave(nc.scalar.copy, upper[:], raw[:, :, HALF:T])
-                nc.gpsimd.tensor_copy(lower[:, 0:HELPER_SHARE, :], raw[:, :, 0:HELPER_SHARE].rearrange("p t n -> p n t"))
-                interleave(nc.scalar.copy, lower[:, HELPER_SHARE:HALF, :], raw[:, :, HELPER_SHARE:HALF])
+            for lo, grouped, helper, own in ((HALF, upper, 0, VECTOR_UPPER[a]), (0, lower, GPSIMD_LOWER[a], VECTOR_LOWER[a])):
+                rows = raw[:, :, lo:lo + HALF]
+                if helper:
+                    nc.gpsimd.tensor_copy(grouped[:, 0:helper, :], rows[:, :, 0:helper].rearrange("p t n -> p n t"))
+                if own:
+                    interleave(nc.vector.tensor_copy, grouped[:, helper:helper + own, :], rows[:, :, helper:helper + own])
+                if helper + own < HALF:
+                    interleave(nc.scalar.copy, grouped[:, helper + own:HALF, :], rows[:, :, helper + own:HALF])
 
-            for lo, grouped in ((HALF, upper), (0, lower)):
+            calls = [(HALF, upper, 0, HALF)]
+            calls += [(0, lower, 0, HALF // 2), (0, lower, HALF // 2, HALF)] if a == PASSES - 1 else [(0, lower, 0, HALF)]
+            for base, grouped, lo, hi in calls:
                 nc.vector.quantize_mx(
-                    out=token_words[:, lo:lo + HALF].bitcast(FP8X4),
-                    scales=token_scales[g][first:P, lo:lo + HALF],
-                    in_=grouped[:].rearrange("p n t -> p (n t)"),
+                    out=token_words[:, base + lo:base + hi].bitcast(FP8X4),
+                    scales=token_scales[g][first:P, base + lo:base + hi],
+                    in_=grouped[:, lo:hi, :].rearrange("p n t -> p (n t)"),
                 )
 
+            if a >= PLANES_FROM[1]:
+                lo = (a - PLANES_FROM[1]) * C
+                nc.vector.tensor_copy(slot_scales[0][:, lo:lo + C], token_scales[0][:].indirect(entries(lo, lo + C)))
+
             last_pass = a == PASSES - 1
-            planes_done = last_pass or a + 1 in PLANES_FROM
             for lo, hi in ((0, C), (C, SLOTS)) if last_pass else ((0, SLOTS),):
-                if planes_done:
+                if last_pass:
                     nc.vector.tensor_copy(slot_scales[g][:, lo:hi], token_scales[g][:].indirect(entries(lo, hi)))
                 nc.vector.tensor_copy(gathered[:, lo:hi], token_words[:].indirect(entries(lo, hi)))
 

@@ -108,11 +108,16 @@ def tile_routed_moe_kernel(tc, xT, w_words, w_scales, b, gate, offs, out):
                 nc.vector.tensor_copy(gathered[:, lo:hi], token_words[:].indirect(entries(lo, hi)))
 
         scale_rows = w_scales.rearrange("e a q n -> q (e a) n")
-        for quadrant in range(4):
-            nc.sync.dma_start(
-                out=weight_scales[32 * quadrant:32 * quadrant + 4].bitcast(I32),
-                in_=scale_rows[4 * quadrant:4 * quadrant + 4].bitcast(I32),
-            )
+
+        def load_scales(first_expert, end_expert):
+            planes = slice(first_expert * PASSES, end_expert * PASSES)
+            for quadrant in range(4):
+                nc.sync.dma_start(
+                    out=weight_scales[32 * quadrant:32 * quadrant + 4, planes, :].bitcast(I32),
+                    in_=scale_rows[4 * quadrant:4 * quadrant + 4, planes, :].bitcast(I32),
+                )
+
+        load_scales(0, 1)
 
         weights = []
         bias = keep.tile([P, BLOCKS, E], F32, name="bias")
@@ -124,6 +129,7 @@ def tile_routed_moe_kernel(tc, xT, w_words, w_scales, b, gate, offs, out):
             if e == 0:
                 nc.sync.dma_start(out=bias[:], in_=b.rearrange("(h p) e -> p h e", p=P))
                 nc.sync.dma_start(out=gate_rows[:], in_=gate[0:P, :])
+                load_scales(1, E)
 
         results = [keep.tile([P, T], F32, name=f"results{h}") for h in range(BLOCKS)]
         squares = [keep.tile([P, SLOTS], F32, name=f"squares{h}") for h in range(BLOCKS)]
@@ -132,7 +138,8 @@ def tile_routed_moe_kernel(tc, xT, w_words, w_scales, b, gate, offs, out):
             for h in range(BLOCKS):
                 features = slice(h * P, (h + 1) * P)
                 sums = psum.tile([P, C], F32, name=f"sums{e}{h}")
-                for a in reversed(range(PASSES)):
+                order = list(range(PASSES)) if e == 0 else list(reversed(range(PASSES)))
+                for a in order:
                     g, first = plane_of(a)
                     nc.tensor.matmul_mx(
                         out=sums[:],
@@ -140,8 +147,8 @@ def tile_routed_moe_kernel(tc, xT, w_words, w_scales, b, gate, offs, out):
                         lhsT_scale=weight_scales[:, e * PASSES + a, features],
                         rhs=slot_words[a][:, slots].bitcast(FP8X4),
                         rhs_scale=slot_scales[g][first:P, slots],
-                        start=(a == PASSES - 1),
-                        stop=(a == 0),
+                        start=(a == order[0]),
+                        stop=(a == order[-1]),
                     )
                 positive = ring.tile([P, C], F32, name="positive")
                 nc.scalar.activation(positive[:], sums[:], RELU, bias=bias[:, h, e:e + 1])

@@ -29,7 +29,7 @@ PLANES_FROM = (0, 2)
 
 VECTOR_UPPER = (512, 0, 0, 0, 0, 0)
 VECTOR_LOWER = (128, 384, 0, 0, 0, 0)
-GPSIMD_LOWER = (0, 0, 288, 288, 288, 320)
+GPSIMD_LOWER = (0, 0, 320, 320, 320, 320)
 
 
 def tile_routed_moe_kernel(tc, xT, w_words, w_scales, b, gate, offs, out):
@@ -89,7 +89,7 @@ def tile_routed_moe_kernel(tc, xT, w_words, w_scales, b, gate, offs, out):
                     interleave(nc.scalar.copy, grouped[:, helper + own:HALF, :], rows[:, :, helper + own:HALF])
 
             calls = [(HALF, upper, 0, HALF)]
-            calls += [(0, lower, 0, HALF // 2), (0, lower, HALF // 2, HALF)] if a == PASSES - 1 else [(0, lower, 0, HALF)]
+            calls += [(0, lower, 0, HALF // 2), (0, lower, HALF // 2, HALF)] if GPSIMD_LOWER[a] else [(0, lower, 0, HALF)]
             for base, grouped, lo, hi in calls:
                 nc.vector.quantize_mx(
                     out=token_words[:, base + lo:base + hi].bitcast(FP8X4),
@@ -129,7 +129,9 @@ def tile_routed_moe_kernel(tc, xT, w_words, w_scales, b, gate, offs, out):
             if e == 0:
                 nc.sync.dma_start(out=bias[:], in_=b.rearrange("(h p) e -> p h e", p=P))
                 nc.sync.dma_start(out=gate_rows[:], in_=gate[0:P, :])
-                load_scales(1, E)
+                load_scales(1, 2)
+            if e == 1:
+                load_scales(2, E)
 
         results = [keep.tile([P, T], F32, name=f"results{h}") for h in range(BLOCKS)]
         squares = [keep.tile([P, SLOTS], F32, name=f"squares{h}") for h in range(BLOCKS)]
@@ -138,7 +140,7 @@ def tile_routed_moe_kernel(tc, xT, w_words, w_scales, b, gate, offs, out):
             for h in range(BLOCKS):
                 features = slice(h * P, (h + 1) * P)
                 sums = psum.tile([P, C], F32, name=f"sums{e}{h}")
-                order = list(range(PASSES)) if e == 0 else list(reversed(range(PASSES)))
+                order = list(range(PASSES)) if e == 0 and h == 0 else list(reversed(range(PASSES)))
                 for a in order:
                     g, first = plane_of(a)
                     nc.tensor.matmul_mx(

@@ -28,8 +28,9 @@ WINDOW = 1408
 PLANES_FROM = (0, 2)
 
 VECTOR_UPPER = (512, 0, 0, 0, 0, 0)
-VECTOR_LOWER = (128, 384, 0, 0, 0, 0)
-GPSIMD_LOWER = (0, 0, 320, 320, 320, 320)
+VECTOR_LOWER = (128, 0, 0, 0, 0, 0)
+GPSIMD_LOWER = (0, 320, 320, 320, 320, 320)
+LAST_LOAD = 768
 
 
 def tile_routed_moe_kernel(tc, xT, w_words, w_scales, b, gate, offs, out):
@@ -73,7 +74,11 @@ def tile_routed_moe_kernel(tc, xT, w_words, w_scales, b, gate, offs, out):
             g, first = plane_of(a)
 
             raw = loads.tile([P, 4, T], F32, name="raw", align_bytes=64)
-            nc.sync.dma_start(out=raw[:], in_=x_passes[a])
+            if a == PASSES - 1:
+                nc.sync.dma_start(out=raw[:, :, 0:LAST_LOAD], in_=x_passes[a][:, :, 0:LAST_LOAD])
+                nc.sync.dma_start(out=raw[:, :, LAST_LOAD:T], in_=x_passes[a][:, :, LAST_LOAD:T])
+            else:
+                nc.sync.dma_start(out=raw[:], in_=x_passes[a])
             if a == 0:
                 nc.sync.dma_start(offsets[:], offs)
 
@@ -85,11 +90,16 @@ def tile_routed_moe_kernel(tc, xT, w_words, w_scales, b, gate, offs, out):
                     nc.gpsimd.tensor_copy(grouped[:, 0:helper, :], rows[:, :, 0:helper].rearrange("p t n -> p n t"))
                 if own:
                     interleave(nc.vector.tensor_copy, grouped[:, helper:helper + own, :], rows[:, :, helper:helper + own])
-                if helper + own < HALF:
-                    interleave(nc.scalar.copy, grouped[:, helper + own:HALF, :], rows[:, :, helper + own:HALF])
+                end = LAST_LOAD - HALF if a == PASSES - 1 and lo == HALF else HALF
+                if helper + own < end:
+                    interleave(nc.scalar.copy, grouped[:, helper + own:end, :], rows[:, :, helper + own:end])
+            if a == PASSES - 1:
+                interleave(nc.scalar.copy, upper[:, LAST_LOAD - HALF:HALF, :], raw[:, :, LAST_LOAD:T])
 
             calls = [(HALF, upper, 0, HALF)]
             calls += [(0, lower, 0, HALF // 2), (0, lower, HALF // 2, HALF)] if GPSIMD_LOWER[a] else [(0, lower, 0, HALF)]
+            if a == PASSES - 1:
+                calls = [(0, lower, 0, HALF), (HALF, upper, 0, HALF)]
             for base, grouped, lo, hi in calls:
                 nc.vector.quantize_mx(
                     out=token_words[:, base + lo:base + hi].bitcast(FP8X4),

@@ -21,21 +21,25 @@ RELU = mybir.ActivationFunctionType.Relu
 SQUARE = mybir.ActivationFunctionType.Square
 MULT = mybir.AluOpType.mult
 
-HALF = T // 2
-
 WINDOW = 1408
 
 PLANES_FROM = (0, 2)
 
-VECTOR_UPPER = (512, 0, 0, 0, 0, 0)
-VECTOR_LOWER = (128, 0, 0, 0, 0, 0)
-GPSIMD_LOWER = (0, 320, 320, 320, 320, 320)
-LAST_LOAD = 768
+SHARED = 384
+PLAN = (
+    (1, 512, (("v", 0, 384), ("s", 384, 512), ("v", 512, 768), ("s", 768, 896), ("s", 896, 1024)), ((0, 256), (256, 384), (384, 896), (896, 1024)), None),
+    (1, 512, (("g", 0, 320), ("s", 384, 512), ("s", 512, 896), ("s", 896, 1024), ("s", 320, 384)), ((384, 896), (896, 1024), (0, 256), (256, 384)), (0, 416)),
+    (1, 512, (("g", 0, 320), ("s", 384, 512), ("s", 512, 896), ("s", 896, 1024), ("s", 320, 384)), ((384, 896), (896, 1024), (0, 256), (256, 384)), (416, 832)),
+    (1, 512, (("g", 0, 320), ("s", 384, 512), ("s", 512, 896), ("s", 896, 1024), ("s", 320, 384)), ((384, 896), (896, 1024), (0, 256), (256, 384)), (832, 1024)),
+    (2, 608, (("g", 0, 320), ("s", 384, 608), ("s", 608, 896), ("s", 896, 1024), ("s", 320, 384)), ((384, 896), (896, 1024), (0, 256), (256, 384)), None),
+    (3, 672, (("g", 0, 288), ("s", 384, 672), ("s", 672, 896), ("v", 896, 1024), ("s", 288, 384)), ((384, 896), (896, 1024), (0, 256), (256, 384)), None),
+)
 
 
 def tile_routed_moe_kernel(tc, xT, w_words, w_scales, b, gate, offs, out):
     nc = tc.nc
     x_passes = xT.rearrange("(a p t) n -> a p t n", p=P, t=4)
+    x_runs = xT.rearrange("(a p t) n -> a p (t n)", p=P, t=4)
 
     with ExitStack() as ctx:
         keep = ctx.enter_context(tc.tile_pool(name="keep", bufs=1))
@@ -73,43 +77,41 @@ def tile_routed_moe_kernel(tc, xT, w_words, w_scales, b, gate, offs, out):
             slot_words.append(gathered)
             g, first = plane_of(a)
 
-            raw = loads.tile([P, 4, T], F32, name="raw", align_bytes=64)
-            if a == PASSES - 1:
-                nc.sync.dma_start(out=raw[:, :, 0:LAST_LOAD], in_=x_passes[a][:, :, 0:LAST_LOAD])
-                nc.sync.dma_start(out=raw[:, :, LAST_LOAD:T], in_=x_passes[a][:, :, LAST_LOAD:T])
+            late_rows, early, copies, calls, filler = PLAN[a]
+            raw = loads.tile([P, 4 * T], F32, name="raw", align_bytes=64)
+            rows = raw[:].rearrange("p (t n) -> p t n", t=4)
+            first_late = 4 - late_rows
+            if late_rows == 0:
+                nc.sync.dma_start(out=raw[:], in_=x_runs[a])
             else:
-                nc.sync.dma_start(out=raw[:], in_=x_passes[a])
+                run = first_late * T + early
+                nc.sync.dma_start(out=raw[:, 0:run], in_=x_runs[a][:, 0:run])
+                if late_rows > 1:
+                    nc.sync.dma_start(out=rows[:, first_late + 1:4, 0:early], in_=x_passes[a][:, first_late + 1:4, 0:early])
+                nc.sync.dma_start(out=rows[:, first_late:4, early:T], in_=x_passes[a][:, first_late:4, early:T])
             if a == 0:
                 nc.sync.dma_start(offsets[:], offs)
 
-            upper = ring.tile([P, HALF, 4], BF16, name="upper", align_bytes=64)
-            lower = single.tile([P, HALF, 4], BF16, name="lower", align_bytes=64)
-            for lo, grouped, helper, own in ((HALF, upper, 0, VECTOR_UPPER[a]), (0, lower, GPSIMD_LOWER[a], VECTOR_LOWER[a])):
-                rows = raw[:, :, lo:lo + HALF]
-                if helper:
-                    nc.gpsimd.tensor_copy(grouped[:, 0:helper, :], rows[:, :, 0:helper].rearrange("p t n -> p n t"))
-                if own:
-                    interleave(nc.vector.tensor_copy, grouped[:, helper:helper + own, :], rows[:, :, helper:helper + own])
-                end = LAST_LOAD - HALF if a == PASSES - 1 and lo == HALF else HALF
-                if helper + own < end:
-                    interleave(nc.scalar.copy, grouped[:, helper + own:end, :], rows[:, :, helper + own:end])
-            if a == PASSES - 1:
-                interleave(nc.scalar.copy, upper[:, LAST_LOAD - HALF:HALF, :], raw[:, :, LAST_LOAD:T])
+            shared = single.tile([P, SHARED, 4], BF16, name="shared", align_bytes=64)
+            others = ring.tile([P, T - SHARED, 4], BF16, name="others", align_bytes=64)
 
-            calls = [(HALF, upper, 0, HALF)]
-            calls += [(0, lower, 0, HALF // 2), (0, lower, HALF // 2, HALF)] if GPSIMD_LOWER[a] else [(0, lower, 0, HALF)]
-            if a == PASSES - 1:
-                calls = [(0, lower, 0, HALF), (HALF, upper, 0, HALF)]
-            for base, grouped, lo, hi in calls:
+            def grouped(lo, hi):
+                return shared[:, lo:hi, :] if hi <= SHARED else others[:, lo - SHARED:hi - SHARED, :]
+
+            for engine, lo, hi in copies:
+                if engine == "g":
+                    nc.gpsimd.tensor_copy(grouped(lo, hi), rows[:, :, lo:hi].rearrange("p t n -> p n t"))
+                else:
+                    interleave(nc.vector.tensor_copy if engine == "v" else nc.scalar.copy, grouped(lo, hi), rows[:, :, lo:hi])
+            for lo, hi in calls:
                 nc.vector.quantize_mx(
-                    out=token_words[:, base + lo:base + hi].bitcast(FP8X4),
-                    scales=token_scales[g][first:P, base + lo:base + hi],
-                    in_=grouped[:, lo:hi, :].rearrange("p n t -> p (n t)"),
+                    out=token_words[:, lo:hi].bitcast(FP8X4),
+                    scales=token_scales[g][first:P, lo:hi],
+                    in_=grouped(lo, hi).rearrange("p n t -> p (n t)"),
                 )
-
-            if a >= PLANES_FROM[1]:
-                lo = (a - PLANES_FROM[1]) * C
-                nc.vector.tensor_copy(slot_scales[0][:, lo:lo + C], token_scales[0][:].indirect(entries(lo, lo + C)))
+            if filler:
+                lo, hi = filler
+                nc.vector.tensor_copy(slot_scales[0][:, lo:hi], token_scales[0][:].indirect(entries(lo, hi)))
 
             last_pass = a == PASSES - 1
             for lo, hi in ((0, C), (C, SLOTS)) if last_pass else ((0, SLOTS),):

@@ -26,13 +26,14 @@ WINDOW = 1408
 PLANES_FROM = (0, 2)
 
 SHARED = 384
+HELD = 192
 PLAN = (
     (1, 512, (("v", 0, 384), ("s", 384, 512), ("v", 512, 768), ("s", 768, 896), ("s", 896, 1024)), ((0, 256), (256, 384), (384, 896), (896, 1024)), None),
-    (1, 512, (("g", 0, 320), ("s", 384, 512), ("s", 512, 896), ("s", 896, 1024), ("s", 320, 384)), ((384, 896), (896, 1024), (0, 256), (256, 384)), (0, 416)),
-    (1, 512, (("g", 0, 320), ("s", 384, 512), ("s", 512, 896), ("s", 896, 1024), ("s", 320, 384)), ((384, 896), (896, 1024), (0, 256), (256, 384)), (416, 832)),
-    (1, 512, (("g", 0, 320), ("s", 384, 512), ("s", 512, 896), ("s", 896, 1024), ("s", 320, 384)), ((384, 896), (896, 1024), (0, 256), (256, 384)), (832, 1024)),
+    (3, 640, (("g", 0, 192), ("s", 384, 640), ("s", 192, 384), ("v", 640, 896), ("s", 896, 1024)), ((0, 256), (256, 384), (384, 896), (896, 1024)), (0, 1024)),
+    (1, 512, (("g", 0, 384), ("s", 384, 512), ("s", 512, 896), ("s", 896, 1024)), ((384, 896), (896, 1024), (0, 256), (256, 384)), None),
+    (1, 512, (("g", 0, 320), ("s", 384, 512), ("s", 512, 896), ("s", 896, 1024), ("s", 320, 384)), ((384, 896), (896, 1024), (0, 256), (256, 384)), None),
     (2, 608, (("g", 0, 320), ("s", 384, 608), ("s", 608, 896), ("s", 896, 1024), ("s", 320, 384)), ((384, 896), (896, 1024), (0, 256), (256, 384)), None),
-    (3, 672, (("g", 0, 288), ("s", 384, 672), ("s", 672, 896), ("v", 896, 1024), ("s", 288, 384)), ((384, 896), (896, 1024), (0, 256), (256, 384)), None),
+    (4, 672, (("g", 0, 320), ("s", 384, 672), ("s", 672, 896), ("s", 896, 1024), ("s", 320, 384)), ((384, 896), (896, 1024), (0, 256), (256, 384)), None),
 )
 
 
@@ -71,6 +72,7 @@ def tile_routed_moe_kernel(tc, xT, w_words, w_scales, b, gate, offs, out):
         def interleave(copy, grouped, raw):
             copy(grouped.rearrange("p (c i) t -> p c t i", i=4), raw.rearrange("p t (c i) -> p c t i", i=4))
 
+        held = None
         for a in range(PASSES):
             token_words = ring.tile([P, WINDOW], U32, name="token_words", align_bytes=64)
             gathered = keep.tile([P, SLOTS], U32, name=f"slot_words{a}", align_bytes=64)
@@ -109,12 +111,15 @@ def tile_routed_moe_kernel(tc, xT, w_words, w_scales, b, gate, offs, out):
                     scales=token_scales[g][first:P, lo:hi],
                     in_=grouped(lo, hi).rearrange("p n t -> p (n t)"),
                 )
+            if held:
+                nc.vector.tensor_copy(held[0][:, SLOTS - HELD:SLOTS], held[1][:].indirect(entries(SLOTS - HELD, SLOTS)))
+            held = (gathered, token_words)
             if filler:
                 lo, hi = filler
                 nc.vector.tensor_copy(slot_scales[0][:, lo:hi], token_scales[0][:].indirect(entries(lo, hi)))
 
             last_pass = a == PASSES - 1
-            for lo, hi in ((0, C), (C, SLOTS)) if last_pass else ((0, SLOTS),):
+            for lo, hi in ((0, C), (C, SLOTS)) if last_pass else ((0, SLOTS - HELD),):
                 if last_pass:
                     nc.vector.tensor_copy(slot_scales[g][:, lo:hi], token_scales[g][:].indirect(entries(lo, hi)))
                 nc.vector.tensor_copy(gathered[:, lo:hi], token_words[:].indirect(entries(lo, hi)))

@@ -28,12 +28,12 @@ PLANES_FROM = (0, 2)
 SHARED = 384
 HELD = 192
 PLAN = (
-    (1, 512, (("v", 0, 384), ("s", 384, 512), ("v", 512, 768), ("s", 768, 896), ("s", 896, 1024)), ((0, 256), (256, 384), (384, 896), (896, 1024)), None),
-    (3, 640, (("g", 0, 192), ("s", 384, 640), ("s", 192, 384), ("v", 640, 896), ("s", 896, 1024)), ((0, 256), (256, 384), (384, 896), (896, 1024)), (0, 1024)),
+    (1, 512, (("v", 0, 384), ("s", 384, 512), ("v", 512, 704), ("s", 704, 896), ("s", 896, 1024)), ((0, 256), (256, 384), (384, 896), (896, 1024)), None),
+    (4, 640, (("g", 0, 192), ("s", 192, 384), ("s", 384, 640), ("v", 640, 896), ("s", 896, 1024)), ((0, 256), (256, 384), (384, 896), (896, 1024)), (0, 1024)),
     (1, 512, (("g", 0, 384), ("s", 384, 512), ("s", 512, 896), ("s", 896, 1024)), ((384, 896), (896, 1024), (0, 256), (256, 384)), None),
     (1, 512, (("g", 0, 320), ("s", 384, 512), ("s", 512, 896), ("s", 896, 1024), ("s", 320, 384)), ((384, 896), (896, 1024), (0, 256), (256, 384)), None),
-    (2, 608, (("g", 0, 320), ("s", 384, 608), ("s", 608, 896), ("s", 896, 1024), ("s", 320, 384)), ((384, 896), (896, 1024), (0, 256), (256, 384)), None),
-    (4, 672, (("g", 0, 320), ("s", 384, 672), ("s", 672, 896), ("s", 896, 1024), ("s", 320, 384)), ((384, 896), (896, 1024), (0, 256), (256, 384)), None),
+    (2, 640, (("g", 0, 320), ("s", 384, 640), ("s", 640, 896), ("s", 896, 1024), ("s", 320, 384)), ((384, 896), (896, 1024), (0, 256), (256, 384)), None),
+    (4, 640, (("g", 0, 320), ("s", 384, 640), ("s", 640, 896), ("s", 896, 1024), ("s", 320, 384)), ((384, 896), (896, 1024), (0, 256), (256, 384)), None),
 )
 
 
@@ -44,7 +44,7 @@ def tile_routed_moe_kernel(tc, xT, w_words, w_scales, b, gate, offs, out):
 
     with ExitStack() as ctx:
         keep = ctx.enter_context(tc.tile_pool(name="keep", bufs=1))
-        loads = ctx.enter_context(tc.tile_pool(name="loads", bufs=4))
+        loads = ctx.enter_context(tc.tile_pool(name="loads", bufs=6))
         ring = ctx.enter_context(tc.tile_pool(name="ring", bufs=3))
         single = ctx.enter_context(tc.tile_pool(name="single", bufs=1))
         psum = ctx.enter_context(tc.psum_pool(name="psum", bufs=1))
@@ -128,10 +128,10 @@ def tile_routed_moe_kernel(tc, xT, w_words, w_scales, b, gate, offs, out):
 
         def load_scales(first_expert, end_expert):
             planes = slice(first_expert * PASSES, end_expert * PASSES)
-            for quadrant in range(4):
+            for row in range(4):
                 nc.sync.dma_start(
-                    out=weight_scales[32 * quadrant:32 * quadrant + 4, planes, :].bitcast(I32),
-                    in_=scale_rows[4 * quadrant:4 * quadrant + 4, planes, :].bitcast(I32),
+                    out=weight_scales[row:P:32, planes, :].bitcast(I32),
+                    in_=scale_rows[row:16:4, planes, :].bitcast(I32),
                 )
 
         load_scales(0, 1)
@@ -145,9 +145,10 @@ def tile_routed_moe_kernel(tc, xT, w_words, w_scales, b, gate, offs, out):
             weights.append(codes)
             if e == 0:
                 nc.sync.dma_start(out=bias[:], in_=b.rearrange("(h p) e -> p h e", p=P))
-                nc.sync.dma_start(out=gate_rows[:], in_=gate[0:P, :])
+                nc.sync.dma_start(out=gate_rows[:, 0:C], in_=gate[0:P, 0:C])
                 load_scales(1, 2)
             if e == 1:
+                nc.sync.dma_start(out=gate_rows[:, C:SLOTS], in_=gate[0:P, C:SLOTS])
                 load_scales(2, E)
 
         results = [keep.tile([P, T], F32, name=f"results{h}") for h in range(BLOCKS)]

@@ -25,15 +25,15 @@ WINDOW = 1408
 
 PLANES_FROM = (0, 2)
 
-SHARED = 384
+SHARED = ((0, 384), (0, 384), (0, 384), (0, 384), (256, 768), (0, 384))
 HELD = 192
 PLAN = (
     (1, 512, (("v", 0, 384), ("s", 384, 512), ("v", 512, 704), ("s", 704, 896), ("s", 896, 1024)), ((0, 256), (256, 384), (384, 896), (896, 1024)), None),
-    (4, 640, (("g", 0, 192), ("s", 192, 384), ("s", 384, 640), ("v", 640, 896), ("s", 896, 1024)), ((0, 256), (256, 384), (384, 896), (896, 1024)), (0, 1024)),
+    (4, 640, (("g", 0, 192), ("s", 192, 384), ("s", 384, 640), ("v", 768, 1024), ("s", 640, 768)), ((0, 256), (256, 384), (384, 640), (640, 768), (768, 1024)), (0, 1024)),
     (1, 512, (("g", 0, 384), ("s", 384, 512), ("s", 512, 896), ("s", 896, 1024)), ((384, 896), (896, 1024), (0, 256), (256, 384)), None),
     (1, 512, (("g", 0, 320), ("s", 384, 512), ("s", 512, 896), ("s", 896, 1024), ("s", 320, 384)), ((384, 896), (896, 1024), (0, 256), (256, 384)), None),
-    (2, 640, (("g", 0, 320), ("s", 384, 640), ("s", 640, 896), ("s", 896, 1024), ("s", 320, 384)), ((384, 896), (896, 1024), (0, 256), (256, 384)), None),
-    (4, 640, (("g", 0, 320), ("s", 384, 640), ("s", 640, 896), ("s", 896, 1024), ("s", 320, 384)), ((384, 896), (896, 1024), (0, 256), (256, 384)), None),
+    (2, 640, (("g", 320, 640), ("s", 0, 256), ("s", 256, 320), ("s", 768, 1024), ("s", 640, 768)), ((0, 256), (256, 512), (768, 1024), (512, 640), (640, 768)), None),
+    (4, 640, (("g", 0, 320), ("s", 384, 640), ("s", 320, 384), ("s", 640, 896), ("s", 896, 1024)), ((0, 256), (256, 384), (384, 640), (640, 896), (896, 1024)), None),
 )
 
 
@@ -70,7 +70,7 @@ def tile_routed_moe_kernel(tc, xT, w_words, w_scales, b, gate, offs, out):
             return g, 4 * (a - PLANES_FROM[g])
 
         def interleave(copy, grouped, raw):
-            copy(grouped.rearrange("p (c i) t -> p c t i", i=4), raw.rearrange("p t (c i) -> p c t i", i=4))
+            copy(grouped.rearrange("p (c i) (u e) -> p c u i e", i=4, u=2), raw.rearrange("p (u e) (c i) -> p c u i e", i=4, u=2))
 
         held = None
         for a in range(PASSES):
@@ -94,11 +94,12 @@ def tile_routed_moe_kernel(tc, xT, w_words, w_scales, b, gate, offs, out):
             if a == 0:
                 nc.sync.dma_start(offsets[:], offs)
 
-            shared = single.tile([P, SHARED, 4], BF16, name="shared", align_bytes=64)
-            others = ring.tile([P, T - SHARED, 4], BF16, name="others", align_bytes=64)
+            shared_lo, shared_hi = SHARED[a]
+            shared = single.tile([P, shared_hi - shared_lo, 4], BF16, name="shared", align_bytes=64)
+            others = ring.tile([P, T, 4], BF16, name="others", align_bytes=64)
 
             def grouped(lo, hi):
-                return shared[:, lo:hi, :] if hi <= SHARED else others[:, lo - SHARED:hi - SHARED, :]
+                return shared[:, lo - shared_lo:hi - shared_lo, :] if shared_lo <= lo and hi <= shared_hi else others[:, lo:hi, :]
 
             for engine, lo, hi in copies:
                 if engine == "g":

@@ -70,7 +70,7 @@ def tile_routed_moe_kernel(tc, xT, w_words, w_scales, b, gate, offs, out):
             return g, 4 * (a - PLANES_FROM[g])
 
         def interleave(copy, grouped, raw):
-            copy(grouped.rearrange("p (c i) (u e) -> p c u i e", i=4, u=2), raw.rearrange("p (u e) (c i) -> p c u i e", i=4, u=2))
+            copy(grouped.rearrange("p (c i) t -> p c t i", i=4), raw.rearrange("p t (c i) -> p c t i", i=4))
 
         held = None
         for a in range(PASSES):
@@ -174,8 +174,8 @@ def tile_routed_moe_kernel(tc, xT, w_words, w_scales, b, gate, offs, out):
                 positive = ring.tile([P, C], F32, name="positive")
                 nc.scalar.activation(positive[:], sums[:], RELU, bias=bias[:, h, e:e + 1])
                 nc.scalar.activation(squares[h][:, slots], positive[:], SQUARE)
-                nc.vector.tensor_tensor(
-                    results[h][:].indirect(entries(slots.start, slots.stop)), squares[h][:, slots], gate_rows[:, slots], MULT
-                )
+                gated = ring.tile([P, C], F32, name="gated")
+                nc.vector.tensor_tensor(gated[:], squares[h][:, slots], gate_rows[:, slots], MULT)
+                nc.vector.tensor_copy(results[h][:].indirect(entries(slots.start, slots.stop)), gated[:])
                 if e == E - 1:
                     nc.sync.dma_start(out=out[features, :], in_=results[h][:])

@@ -25,15 +25,13 @@ WINDOW = 1408
 
 PLANES_FROM = (0, 2)
 
-SHARED = ((0, 384), (0, 384), (0, 384), (0, 384), (256, 768), (0, 384))
-HELD = 192
 PLAN = (
-    (1, 512, (("v", 0, 384), ("s", 384, 512), ("v", 512, 704), ("s", 704, 896), ("s", 896, 1024)), ((0, 256), (256, 384), (384, 896), (896, 1024)), None),
-    (4, 640, (("g", 0, 192), ("s", 192, 384), ("s", 384, 640), ("v", 768, 1024), ("s", 640, 768)), ((0, 256), (256, 384), (384, 640), (640, 768), (768, 1024)), (0, 1024)),
-    (1, 512, (("g", 0, 384), ("s", 384, 512), ("s", 512, 896), ("s", 896, 1024)), ((384, 896), (896, 1024), (0, 256), (256, 384)), None),
-    (1, 512, (("g", 0, 320), ("s", 384, 512), ("s", 512, 896), ("s", 896, 1024), ("s", 320, 384)), ((384, 896), (896, 1024), (0, 256), (256, 384)), None),
-    (2, 640, (("g", 320, 640), ("s", 0, 256), ("s", 256, 320), ("s", 768, 1024), ("s", 640, 768)), ((0, 256), (256, 512), (768, 1024), (512, 640), (640, 768)), None),
-    (4, 640, (("g", 0, 320), ("s", 384, 640), ("s", 320, 384), ("s", 640, 896), ("s", 896, 1024)), ((0, 256), (256, 384), (384, 640), (640, 896), (896, 1024)), None),
+    (1, 512, (("v", 0, 384), ("s", 384, 512), ("v", 512, 640), ("s", 640, 768), ("s", 768, 1024)), ((0, 512), (512, 768), (768, 1024))),
+    (1, 512, (("g", 0, 128), ("s", 128, 256), ("s", 256, 512), ("v", 512, 768), ("s", 768, 1024)), ((512, 768), (0, 512), (768, 1024))),
+    (1, 512, (("g", 0, 288), ("s", 288, 512), ("s", 512, 768), ("s", 768, 1024)), ((0, 512), (512, 768), (768, 1024))),
+    (1, 512, (("g", 0, 288), ("s", 288, 512), ("s", 512, 768), ("s", 768, 1024)), ((0, 512), (512, 768), (768, 1024))),
+    (1, 512, (("g", 0, 288), ("s", 288, 512), ("s", 512, 768), ("s", 768, 1024)), ((0, 512), (512, 768), (768, 1024))),
+    (4, (640,), (("g", 0, 288), ("s", 288, 640), ("s", 640, 896), ("s", 896, 1024)), ((0, 512), (512, 640), (640, 896), (896, 1024))),
 )
 
 
@@ -44,7 +42,6 @@ def tile_routed_moe_kernel(tc, xT, w_words, w_scales, b, gate, offs, out):
 
     with ExitStack() as ctx:
         keep = ctx.enter_context(tc.tile_pool(name="keep", bufs=1))
-        loads = ctx.enter_context(tc.tile_pool(name="loads", bufs=6))
         ring = ctx.enter_context(tc.tile_pool(name="ring", bufs=3))
         single = ctx.enter_context(tc.tile_pool(name="single", bufs=1))
         psum = ctx.enter_context(tc.psum_pool(name="psum", bufs=1))
@@ -72,58 +69,59 @@ def tile_routed_moe_kernel(tc, xT, w_words, w_scales, b, gate, offs, out):
         def interleave(copy, grouped, raw):
             copy(grouped.rearrange("p (c i) t -> p c t i", i=4), raw.rearrange("p t (c i) -> p c t i", i=4))
 
-        held = None
         for a in range(PASSES):
             token_words = ring.tile([P, WINDOW], U32, name="token_words", align_bytes=64)
             gathered = keep.tile([P, SLOTS], U32, name=f"slot_words{a}", align_bytes=64)
             slot_words.append(gathered)
             g, first = plane_of(a)
 
-            late_rows, early, copies, calls, filler = PLAN[a]
-            raw = loads.tile([P, 4 * T], F32, name="raw", align_bytes=64)
-            rows = raw[:].rearrange("p (t n) -> p t n", t=4)
-            first_late = 4 - late_rows
-            if late_rows == 0:
-                nc.sync.dma_start(out=raw[:], in_=x_runs[a])
+            late_rows, early, copies, calls = PLAN[a]
+            if late_rows == 4:
+                cuts = (0,) + early + (T,)
+                parts = []
+                for lo, hi in zip(cuts, cuts[1:]):
+                    part = keep.tile([P, 4, hi - lo], F32, name=f"raw{a}_{lo}", align_bytes=64)
+                    nc.sync.dma_start(out=part[:], in_=x_passes[a][:, :, lo:hi])
+                    parts.append((lo, hi, part[:]))
             else:
-                run = first_late * T + early
-                nc.sync.dma_start(out=raw[:, 0:run], in_=x_runs[a][:, 0:run])
-                if late_rows > 1:
-                    nc.sync.dma_start(out=rows[:, first_late + 1:4, 0:early], in_=x_passes[a][:, first_late + 1:4, 0:early])
-                nc.sync.dma_start(out=rows[:, first_late:4, early:T], in_=x_passes[a][:, first_late:4, early:T])
+                raw = keep.tile([P, 4 * T], F32, name=f"raw{a}", align_bytes=64)
+                rows = raw[:].rearrange("p (t n) -> p t n", t=4)
+                first_late = 4 - late_rows
+                if late_rows == 0:
+                    nc.sync.dma_start(out=raw[:], in_=x_runs[a])
+                else:
+                    run = first_late * T + early
+                    nc.sync.dma_start(out=raw[:, 0:run], in_=x_runs[a][:, 0:run])
+                    if late_rows > 1:
+                        nc.sync.dma_start(out=rows[:, first_late + 1:4, 0:early], in_=x_passes[a][:, first_late + 1:4, 0:early])
+                    nc.sync.dma_start(out=rows[:, first_late:4, early:T], in_=x_passes[a][:, first_late:4, early:T])
+                parts = [(0, T, rows)]
             if a == 0:
                 nc.sync.dma_start(offsets[:], offs)
 
-            shared_lo, shared_hi = SHARED[a]
-            shared = single.tile([P, shared_hi - shared_lo, 4], BF16, name="shared", align_bytes=64)
-            others = ring.tile([P, T, 4], BF16, name="others", align_bytes=64)
+            def loaded(lo, hi):
+                return [part[:, :, lo - start:hi - start] for start, end, part in parts if start <= lo and hi <= end][0]
 
-            def grouped(lo, hi):
-                return shared[:, lo - shared_lo:hi - shared_lo, :] if shared_lo <= lo and hi <= shared_hi else others[:, lo:hi, :]
-
+            grouped = single.tile([P, T, 4], BF16, name="grouped", align_bytes=64)
             for engine, lo, hi in copies:
                 if engine == "g":
-                    nc.gpsimd.tensor_copy(grouped(lo, hi), rows[:, :, lo:hi].rearrange("p t n -> p n t"))
+                    nc.gpsimd.tensor_copy(grouped[:, lo:hi, :], loaded(lo, hi).rearrange("p t n -> p n t"))
                 else:
-                    interleave(nc.vector.tensor_copy if engine == "v" else nc.scalar.copy, grouped(lo, hi), rows[:, :, lo:hi])
+                    interleave(nc.vector.tensor_copy if engine == "v" else nc.scalar.copy, grouped[:, lo:hi, :], loaded(lo, hi))
             for lo, hi in calls:
                 nc.vector.quantize_mx(
                     out=token_words[:, lo:hi].bitcast(FP8X4),
                     scales=token_scales[g][first:P, lo:hi],
-                    in_=grouped(lo, hi).rearrange("p n t -> p (n t)"),
+                    in_=grouped[:, lo:hi, :].rearrange("p n t -> p (n t)"),
                 )
-            if held:
-                nc.vector.tensor_copy(held[0][:, SLOTS - HELD:SLOTS], held[1][:].indirect(entries(SLOTS - HELD, SLOTS)))
-            held = (gathered, token_words)
-            if filler:
-                lo, hi = filler
-                nc.vector.tensor_copy(slot_scales[0][:, lo:hi], token_scales[0][:].indirect(entries(lo, hi)))
-
-            last_pass = a == PASSES - 1
-            for lo, hi in ((0, C), (C, SLOTS)) if last_pass else ((0, SLOTS - HELD),):
-                if last_pass:
+            if a < PASSES - 1:
+                nc.vector.tensor_copy(gathered[:], token_words[:].indirect(entries(0, SLOTS)))
+                if a == PLANES_FROM[1] - 1:
+                    nc.vector.tensor_copy(slot_scales[0][:], token_scales[0][:].indirect(entries(0, SLOTS)))
+            else:
+                for lo, hi in ((0, C), (C, SLOTS)):
                     nc.vector.tensor_copy(slot_scales[g][:, lo:hi], token_scales[g][:].indirect(entries(lo, hi)))
-                nc.vector.tensor_copy(gathered[:, lo:hi], token_words[:].indirect(entries(lo, hi)))
+                    nc.vector.tensor_copy(gathered[:, lo:hi], token_words[:].indirect(entries(lo, hi)))
 
         scale_rows = w_scales.rearrange("e a q n -> q (e a) n")
 
@@ -174,8 +172,8 @@ def tile_routed_moe_kernel(tc, xT, w_words, w_scales, b, gate, offs, out):
                 positive = ring.tile([P, C], F32, name="positive")
                 nc.scalar.activation(positive[:], sums[:], RELU, bias=bias[:, h, e:e + 1])
                 nc.scalar.activation(squares[h][:, slots], positive[:], SQUARE)
-                gated = ring.tile([P, C], F32, name="gated")
-                nc.vector.tensor_tensor(gated[:], squares[h][:, slots], gate_rows[:, slots], MULT)
-                nc.vector.tensor_copy(results[h][:].indirect(entries(slots.start, slots.stop)), gated[:])
+                nc.vector.tensor_tensor(
+                    results[h][:].indirect(entries(slots.start, slots.stop)), squares[h][:, slots], gate_rows[:, slots], MULT
+                )
                 if e == E - 1:
                     nc.sync.dma_start(out=out[features, :], in_=results[h][:])

@@ -25,13 +25,14 @@ WINDOW = 1408
 
 PLANES_FROM = (0, 2)
 
+HELD = 192
 PLAN = (
-    (1, 512, (("v", 0, 384), ("s", 384, 512), ("v", 512, 640), ("s", 640, 768), ("s", 768, 1024)), ((0, 512), (512, 768), (768, 1024))),
-    (1, 512, (("g", 0, 128), ("s", 128, 256), ("s", 256, 512), ("v", 512, 768), ("s", 768, 1024)), ((512, 768), (0, 512), (768, 1024))),
-    (1, 512, (("g", 0, 288), ("s", 288, 512), ("s", 512, 768), ("s", 768, 1024)), ((0, 512), (512, 768), (768, 1024))),
-    (1, 512, (("g", 0, 288), ("s", 288, 512), ("s", 512, 768), ("s", 768, 1024)), ((0, 512), (512, 768), (768, 1024))),
-    (1, 512, (("g", 0, 288), ("s", 288, 512), ("s", 512, 768), ("s", 768, 1024)), ((0, 512), (512, 768), (768, 1024))),
-    (4, (640,), (("g", 0, 288), ("s", 288, 640), ("s", 640, 896), ("s", 896, 1024)), ((0, 512), (512, 640), (640, 896), (896, 1024))),
+    (1, 512, ((768, 1024),), (("v", 0, 384), ("s", 384, 512), ("v", 512, 640), ("s", 640, 768), ("s", 768, 1024)), ((0, 512), (512, 768), (768, 1024))),
+    (4, (512, 768), ((0, 256), (896, 1024)), (("g", 0, 256), ("s", 256, 512), ("s", 512, 768), ("s", 768, 896), ("s", 896, 1024)), ((256, 512), (0, 256), (512, 768), (768, 896), (896, 1024))),
+    (1, 512, ((0, 384), (896, 1024)), (("g", 0, 320), ("s", 384, 512), ("s", 512, 896), ("s", 320, 384), ("s", 896, 1024)), ((384, 896), (0, 256), (256, 384), (896, 1024))),
+    (4, (512,), ((0, 256), (896, 1024)), (("g", 0, 256), ("s", 256, 512), ("s", 512, 768), ("s", 768, 896), ("s", 896, 1024)), ((256, 512), (0, 256), (512, 768), (768, 896), (896, 1024))),
+    (4, (512, 768), ((0, 256), (896, 1024)), (("g", 0, 256), ("s", 256, 512), ("s", 512, 768), ("s", 768, 896), ("s", 896, 1024)), ((256, 512), (0, 256), (512, 768), (768, 896), (896, 1024))),
+    (4, (512, 768), ((0, 256), (896, 1024)), (("g", 0, 256), ("s", 256, 512), ("s", 512, 768), ("s", 768, 896), ("s", 896, 1024)), ((256, 512), (0, 256), (512, 768), (768, 896), (896, 1024))),
 )
 
 
@@ -69,13 +70,14 @@ def tile_routed_moe_kernel(tc, xT, w_words, w_scales, b, gate, offs, out):
         def interleave(copy, grouped, raw):
             copy(grouped.rearrange("p (c i) t -> p c t i", i=4), raw.rearrange("p t (c i) -> p c t i", i=4))
 
+        held = None
         for a in range(PASSES):
             token_words = ring.tile([P, WINDOW], U32, name="token_words", align_bytes=64)
             gathered = keep.tile([P, SLOTS], U32, name=f"slot_words{a}", align_bytes=64)
             slot_words.append(gathered)
             g, first = plane_of(a)
 
-            late_rows, early, copies, calls = PLAN[a]
+            late_rows, early, shared_ranges, copies, calls = PLAN[a]
             if late_rows == 4:
                 cuts = (0,) + early + (T,)
                 parts = []
@@ -102,20 +104,33 @@ def tile_routed_moe_kernel(tc, xT, w_words, w_scales, b, gate, offs, out):
             def loaded(lo, hi):
                 return [part[:, :, lo - start:hi - start] for start, end, part in parts if start <= lo and hi <= end][0]
 
-            grouped = single.tile([P, T, 4], BF16, name="grouped", align_bytes=64)
+            shared = single.tile([P, 768, 4], BF16, name="shared", align_bytes=64)
+            others = ring.tile([P, T, 4], BF16, name="others", align_bytes=64)
+
+            def grouped(lo, hi):
+                at = 0
+                for start, end in shared_ranges:
+                    if start <= lo and hi <= end:
+                        return shared[:, at + lo - start:at + hi - start, :]
+                    at += end - start
+                return others[:, lo:hi, :]
+
             for engine, lo, hi in copies:
                 if engine == "g":
-                    nc.gpsimd.tensor_copy(grouped[:, lo:hi, :], loaded(lo, hi).rearrange("p t n -> p n t"))
+                    nc.gpsimd.tensor_copy(grouped(lo, hi), loaded(lo, hi).rearrange("p t n -> p n t"))
                 else:
-                    interleave(nc.vector.tensor_copy if engine == "v" else nc.scalar.copy, grouped[:, lo:hi, :], loaded(lo, hi))
+                    interleave(nc.vector.tensor_copy if engine == "v" else nc.scalar.copy, grouped(lo, hi), loaded(lo, hi))
             for lo, hi in calls:
                 nc.vector.quantize_mx(
                     out=token_words[:, lo:hi].bitcast(FP8X4),
                     scales=token_scales[g][first:P, lo:hi],
-                    in_=grouped[:, lo:hi, :].rearrange("p n t -> p (n t)"),
+                    in_=grouped(lo, hi).rearrange("p n t -> p (n t)"),
                 )
+            if held:
+                nc.vector.tensor_copy(held[0][:, SLOTS - HELD:SLOTS], held[1][:].indirect(entries(SLOTS - HELD, SLOTS)))
+            held = (gathered, token_words)
             if a < PASSES - 1:
-                nc.vector.tensor_copy(gathered[:], token_words[:].indirect(entries(0, SLOTS)))
+                nc.vector.tensor_copy(gathered[:, 0:SLOTS - HELD], token_words[:].indirect(entries(0, SLOTS - HELD)))
                 if a == PLANES_FROM[1] - 1:
                     nc.vector.tensor_copy(slot_scales[0][:], token_scales[0][:].indirect(entries(0, SLOTS)))
             else:

@@ -28,11 +28,11 @@ PLANES_FROM = (0, 2)
 HELD = 192
 PLAN = (
     (1, 512, ((768, 1024),), (("v", 0, 384), ("s", 384, 512), ("v", 512, 640), ("s", 640, 768), ("s", 768, 1024)), ((0, 512), (512, 768), (768, 1024))),
-    (4, (512, 768), ((0, 256), (896, 1024)), (("g", 0, 256), ("s", 256, 512), ("s", 512, 768), ("s", 768, 896), ("s", 896, 1024)), ((256, 512), (0, 256), (512, 768), (768, 896), (896, 1024))),
+    (1, 512, ((896, 1024),), (("v", 0, 256), ("s", 256, 512), ("v", 512, 704), ("s", 704, 896), ("s", 896, 1024)), ((0, 256), (256, 512), (512, 768), (768, 896), (896, 1024))),
     (1, 512, ((0, 384), (896, 1024)), (("g", 0, 320), ("s", 384, 512), ("s", 512, 896), ("s", 320, 384), ("s", 896, 1024)), ((384, 896), (0, 256), (256, 384), (896, 1024))),
-    (4, (512,), ((0, 256), (896, 1024)), (("g", 0, 256), ("s", 256, 512), ("s", 512, 768), ("s", 768, 896), ("s", 896, 1024)), ((256, 512), (0, 256), (512, 768), (768, 896), (896, 1024))),
-    (4, (512, 768), ((0, 256), (896, 1024)), (("g", 0, 256), ("s", 256, 512), ("s", 512, 768), ("s", 768, 896), ("s", 896, 1024)), ((256, 512), (0, 256), (512, 768), (768, 896), (896, 1024))),
-    (4, (512, 768), ((0, 256), (896, 1024)), (("g", 0, 256), ("s", 256, 512), ("s", 512, 768), ("s", 768, 896), ("s", 896, 1024)), ((256, 512), (0, 256), (512, 768), (768, 896), (896, 1024))),
+    (1, 512, ((0, 384), (896, 1024)), (("g", 0, 256), ("s", 384, 512), ("s", 512, 896), ("s", 256, 384), ("s", 896, 1024)), ((384, 896), (0, 256), (256, 384), (896, 1024))),
+    (1, 512, ((0, 384), (896, 1024)), (("g", 0, 288), ("s", 384, 512), ("s", 512, 896), ("s", 288, 384), ("s", 896, 1024)), ((384, 896), (0, 256), (256, 384), (896, 1024))),
+    (4, (640,), ((0, 256),), (("g", 0, 256), ("s", 256, 640), ("s", 640, 896), ("s", 896, 1024)), ((0, 256), (256, 512), (512, 640), (640, 896), (896, 1024))),
 )
 
 

@@ -25,7 +25,7 @@ WINDOW = 1408
 
 PLANES_FROM = (0, 2)
 
-HELD = 192
+HELD = 128
 PLAN = (
     (1, 512, ((768, 1024),), (("v", 0, 384), ("s", 384, 512), ("v", 512, 640), ("s", 640, 768), ("s", 768, 1024)), ((0, 512), (512, 768), (768, 1024))),
     (1, 512, ((896, 1024),), (("v", 0, 256), ("s", 256, 512), ("v", 512, 704), ("s", 704, 896), ("s", 896, 1024)), ((0, 256), (256, 512), (512, 768), (768, 896), (896, 1024))),
@@ -62,6 +62,7 @@ def tile_routed_moe_kernel(tc, xT, w_words, w_scales, b, gate, offs, out):
 
         slot_scales = [keep.tile([P, SLOTS], U8, name=f"slot_scales{g}", align_bytes=64) for g in range(len(PLANES_FROM))]
         slot_words = []
+        held_words = []
 
         def plane_of(a):
             g = len([start for start in PLANES_FROM if start <= a]) - 1
@@ -73,7 +74,7 @@ def tile_routed_moe_kernel(tc, xT, w_words, w_scales, b, gate, offs, out):
         held = None
         for a in range(PASSES):
             token_words = ring.tile([P, WINDOW], U32, name="token_words", align_bytes=64)
-            gathered = keep.tile([P, SLOTS], U32, name=f"slot_words{a}", align_bytes=64)
+            gathered = keep.tile([P, SLOTS if a == PASSES - 1 else SLOTS - HELD], U32, name=f"slot_words{a}", align_bytes=64)
             slot_words.append(gathered)
             g, first = plane_of(a)
 
@@ -82,11 +83,13 @@ def tile_routed_moe_kernel(tc, xT, w_words, w_scales, b, gate, offs, out):
                 cuts = (0,) + early + (T,)
                 parts = []
                 for lo, hi in zip(cuts, cuts[1:]):
-                    part = keep.tile([P, 4, hi - lo], F32, name=f"raw{a}_{lo}", align_bytes=64)
+                    last_tag = f"raw{a}_{lo}"
+                    part = keep.tile([P, 4, hi - lo], F32, name=last_tag, tag=last_tag, align_bytes=64)
                     nc.sync.dma_start(out=part[:], in_=x_passes[a][:, :, lo:hi])
                     parts.append((lo, hi, part[:]))
             else:
-                raw = keep.tile([P, 4 * T], F32, name=f"raw{a}", align_bytes=64)
+                last_tag = f"raw{a}"
+                raw = keep.tile([P, 4 * T], F32, name=last_tag, tag=last_tag, align_bytes=64)
                 rows = raw[:].rearrange("p (t n) -> p t n", t=4)
                 first_late = 4 - late_rows
                 if late_rows == 0:
@@ -126,11 +129,13 @@ def tile_routed_moe_kernel(tc, xT, w_words, w_scales, b, gate, offs, out):
                     scales=token_scales[g][first:P, lo:hi],
                     in_=grouped(lo, hi).rearrange("p n t -> p (n t)"),
                 )
-            if held:
-                nc.vector.tensor_copy(held[0][:, SLOTS - HELD:SLOTS], held[1][:].indirect(entries(SLOTS - HELD, SLOTS)))
-            held = (gathered, token_words)
+            if a > 0:
+                rest = keep.tile([P, HELD], U32, name=f"held_words{a}", tag=last_tag, align_bytes=64)
+                nc.vector.tensor_copy(rest[:], held[:, 0:T].indirect(entries(SLOTS - HELD, SLOTS)))
+                held_words.append(rest)
+            held = token_words
             if a < PASSES - 1:
-                nc.vector.tensor_copy(gathered[:, 0:SLOTS - HELD], token_words[:].indirect(entries(0, SLOTS - HELD)))
+                nc.vector.tensor_copy(gathered[:], token_words[:].indirect(entries(0, SLOTS - HELD)))
                 if a == PLANES_FROM[1] - 1:
                     nc.vector.tensor_copy(slot_scales[0][:], token_scales[0][:].indirect(entries(0, SLOTS)))
             else:
@@ -173,17 +178,20 @@ def tile_routed_moe_kernel(tc, xT, w_words, w_scales, b, gate, offs, out):
                 features = slice(h * P, (h + 1) * P)
                 sums = psum.tile([P, C], F32, name=f"sums{e}{h}")
                 order = list(range(PASSES)) if e == 0 and h == 0 else list(reversed(range(PASSES)))
-                for a in order:
-                    g, first = plane_of(a)
-                    nc.tensor.matmul_mx(
-                        out=sums[:],
-                        lhsT=weights[e][:, a, features].bitcast(FP8X4),
-                        lhsT_scale=weight_scales[:, e * PASSES + a, features],
-                        rhs=slot_words[a][:, slots].bitcast(FP8X4),
-                        rhs_scale=slot_scales[g][first:P, slots],
-                        start=(a == order[0]),
-                        stop=(a == order[-1]),
-                    )
+                cuts = (slots.start, SLOTS - HELD, SLOTS) if e == E - 1 else (slots.start, slots.stop)
+                for lo, hi in zip(cuts, cuts[1:]):
+                    for a in order:
+                        g, first = plane_of(a)
+                        words = held_words[a][:] if lo == SLOTS - HELD and a < PASSES - 1 else slot_words[a][:, lo:hi]
+                        nc.tensor.matmul_mx(
+                            out=sums[:, lo - slots.start:hi - slots.start],
+                            lhsT=weights[e][:, a, features].bitcast(FP8X4),
+                            lhsT_scale=weight_scales[:, e * PASSES + a, features],
+                            rhs=words.bitcast(FP8X4),
+                            rhs_scale=slot_scales[g][first:P, lo:hi],
+                            start=(a == order[0]),
+                            stop=(a == order[-1]),
+                        )
                 positive = ring.tile([P, C], F32, name="positive")
                 nc.scalar.activation(positive[:], sums[:], RELU, bias=bias[:, h, e:e + 1])
                 nc.scalar.activation(squares[h][:, slots], positive[:], SQUARE)

@@ -27,12 +27,12 @@ PLANES_FROM = (0, 2)
 
 HELD = 128
 PLAN = (
-    (1, 512, ((768, 1024),), (("v", 0, 384), ("s", 384, 512), ("v", 512, 640), ("s", 640, 768), ("s", 768, 1024)), ((0, 512), (512, 768), (768, 1024))),
-    (1, 512, ((896, 1024),), (("v", 0, 256), ("s", 256, 512), ("v", 512, 704), ("s", 704, 896), ("s", 896, 1024)), ((0, 256), (256, 512), (512, 768), (768, 896), (896, 1024))),
-    (1, 512, ((0, 384), (896, 1024)), (("g", 0, 320), ("s", 384, 512), ("s", 512, 896), ("s", 320, 384), ("s", 896, 1024)), ((384, 896), (0, 256), (256, 384), (896, 1024))),
-    (1, 512, ((0, 384), (896, 1024)), (("g", 0, 256), ("s", 384, 512), ("s", 512, 896), ("s", 256, 384), ("s", 896, 1024)), ((384, 896), (0, 256), (256, 384), (896, 1024))),
-    (1, 512, ((0, 384), (896, 1024)), (("g", 0, 288), ("s", 384, 512), ("s", 512, 896), ("s", 288, 384), ("s", 896, 1024)), ((384, 896), (0, 256), (256, 384), (896, 1024))),
-    (4, (640,), ((0, 256),), (("g", 0, 256), ("s", 256, 640), ("s", 640, 896), ("s", 896, 1024)), ((0, 256), (256, 512), (512, 640), (640, 896), (896, 1024))),
+    (0, (3584,), ((896, 1024),), (("v", 0, 384, 0, 4), ("s", 384, 512, 0, 4), ("v", 512, 704, 0, 4), ("s", 704, 896, 0, 4), ("s", 896, 1024, 0, 4),), ((0, 256), (256, 384), (384, 896), (896, 1024),)),
+    (0, (3584,), ((896, 1024),), (("v", 0, 320, 0, 4), ("s", 320, 512, 0, 4), ("v", 512, 704, 0, 4), ("s", 704, 896, 0, 4), ("s", 896, 1024, 0, 4),), ((0, 256), (256, 512), (512, 768), (768, 896), (896, 1024),)),
+    (0, (3584,), ((0, 384), (896, 1024),), (("g", 0, 320, 0, 4), ("s", 384, 512, 0, 4), ("s", 512, 896, 0, 4), ("s", 320, 384, 0, 4), ("s", 896, 1024, 0, 4),), ((384, 896), (0, 256), (256, 384), (896, 1024),)),
+    (0, (3584,), ((0, 384), (896, 1024),), (("g", 0, 288, 0, 4), ("s", 288, 384, 0, 4), ("s", 512, 896, 0, 4), ("s", 896, 1024, 0, 4), ("v", 384, 512, 0, 4),), ((0, 256), (256, 384), (384, 896), (896, 1024),)),
+    (0, (3584,), ((0, 384), (896, 1024),), (("g", 0, 288, 0, 4), ("s", 288, 384, 0, 4), ("s", 512, 896, 0, 4), ("s", 896, 1024, 0, 4), ("v", 384, 512, 0, 4),), ((0, 256), (256, 384), (384, 896), (896, 1024),)),
+    (4, (640,), ((0, 384),), (("g", 0, 320, 0, 4), ("s", 384, 640, 0, 4), ("s", 320, 384, 0, 4), ("s", 640, 896, 0, 4), ("v", 896, 1024, 0, 4),), ((0, 256), (256, 384), (384, 640), (896, 1024), (640, 896),)),
 )
 
 
@@ -91,14 +91,15 @@ def tile_routed_moe_kernel(tc, xT, w_words, w_scales, b, gate, offs, out):
                 last_tag = f"raw{a}"
                 raw = keep.tile([P, 4 * T], F32, name=last_tag, tag=last_tag, align_bytes=64)
                 rows = raw[:].rearrange("p (t n) -> p t n", t=4)
-                first_late = 4 - late_rows
                 if late_rows == 0:
-                    nc.sync.dma_start(out=raw[:], in_=x_runs[a])
+                    cuts = (0,) + early + (4 * T,)
+                    for lo, hi in zip(cuts, cuts[1:]):
+                        nc.sync.dma_start(out=raw[:, lo:hi], in_=x_runs[a][:, lo:hi])
                 else:
+                    first_late = 4 - late_rows
                     run = first_late * T + early
                     nc.sync.dma_start(out=raw[:, 0:run], in_=x_runs[a][:, 0:run])
-                    if late_rows > 1:
-                        nc.sync.dma_start(out=rows[:, first_late + 1:4, 0:early], in_=x_passes[a][:, first_late + 1:4, 0:early])
+                    nc.sync.dma_start(out=rows[:, first_late + 1:4, 0:early], in_=x_passes[a][:, first_late + 1:4, 0:early])
                     nc.sync.dma_start(out=rows[:, first_late:4, early:T], in_=x_passes[a][:, first_late:4, early:T])
                 parts = [(0, T, rows)]
             if a == 0:
@@ -118,11 +119,11 @@ def tile_routed_moe_kernel(tc, xT, w_words, w_scales, b, gate, offs, out):
                     at += end - start
                 return others[:, lo:hi, :]
 
-            for engine, lo, hi in copies:
+            for engine, lo, hi, t0, t1 in copies:
                 if engine == "g":
-                    nc.gpsimd.tensor_copy(grouped(lo, hi), loaded(lo, hi).rearrange("p t n -> p n t"))
+                    nc.gpsimd.tensor_copy(grouped(lo, hi)[:, :, t0:t1], loaded(lo, hi)[:, t0:t1, :].rearrange("p t n -> p n t"))
                 else:
-                    interleave(nc.vector.tensor_copy if engine == "v" else nc.scalar.copy, grouped(lo, hi), loaded(lo, hi))
+                    interleave(nc.vector.tensor_copy if engine == "v" else nc.scalar.copy, grouped(lo, hi)[:, :, t0:t1], loaded(lo, hi)[:, t0:t1, :])
             for lo, hi in calls:
                 nc.vector.quantize_mx(
                     out=token_words[:, lo:hi].bitcast(FP8X4),

@@ -25,14 +25,13 @@ WINDOW = 1408
 
 PLANES_FROM = (0, 2)
 
-HELD = 128
 PLAN = (
-    (0, (3584,), ((896, 1024),), (("v", 0, 384, 0, 4), ("s", 384, 512, 0, 4), ("v", 512, 704, 0, 4), ("s", 704, 896, 0, 4), ("s", 896, 1024, 0, 4),), ((0, 256), (256, 384), (384, 896), (896, 1024),)),
-    (0, (3584,), ((896, 1024),), (("v", 0, 320, 0, 4), ("s", 320, 512, 0, 4), ("v", 512, 704, 0, 4), ("s", 704, 896, 0, 4), ("s", 896, 1024, 0, 4),), ((0, 256), (256, 512), (512, 768), (768, 896), (896, 1024),)),
-    (0, (3584,), ((0, 384), (896, 1024),), (("g", 0, 320, 0, 4), ("s", 384, 512, 0, 4), ("s", 512, 896, 0, 4), ("s", 320, 384, 0, 4), ("s", 896, 1024, 0, 4),), ((384, 896), (0, 256), (256, 384), (896, 1024),)),
-    (0, (3584,), ((0, 384), (896, 1024),), (("g", 0, 288, 0, 4), ("s", 288, 384, 0, 4), ("s", 512, 896, 0, 4), ("s", 896, 1024, 0, 4), ("v", 384, 512, 0, 4),), ((0, 256), (256, 384), (384, 896), (896, 1024),)),
-    (0, (3584,), ((0, 384), (896, 1024),), (("g", 0, 288, 0, 4), ("s", 288, 384, 0, 4), ("s", 512, 896, 0, 4), ("s", 896, 1024, 0, 4), ("v", 384, 512, 0, 4),), ((0, 256), (256, 384), (384, 896), (896, 1024),)),
-    (4, (640,), ((0, 384),), (("g", 0, 320, 0, 4), ("s", 384, 640, 0, 4), ("s", 320, 384, 0, 4), ("s", 640, 896, 0, 4), ("v", 896, 1024, 0, 4),), ((0, 256), (256, 384), (384, 640), (896, 1024), (640, 896),)),
+    (0, (3584,), (((512, 1024),),), (("v", 0, 384), ("s", 384, 512), ("v", 512, 768), ("s", 768, 1024), ("q", 0, 512), ("q", 512, 1024),)),
+    (0, (3584,), (((768, 1024),),), (("s", 0, 256), ("v", 256, 768), ("s", 768, 1024), ("q", 0, 256), ("q", 256, 768), ("q", 768, 1024),)),
+    (0, (3584,), (((0, 384), (896, 1024),),), (("g", 0, 288), ("s", 384, 512), ("s", 512, 896), ("s", 288, 384), ("s", 896, 1024), ("q", 384, 896), ("q", 0, 256), ("q", 256, 384), ("q", 896, 1024),)),
+    (0, (3584,), (((0, 384), (896, 1024),),), (("g", 0, 288), ("s", 384, 512), ("s", 512, 896), ("s", 288, 384), ("s", 896, 1024), ("q", 384, 896), ("q", 0, 256), ("q", 256, 384), ("q", 896, 1024),)),
+    (0, (3584,), (((0, 384), (896, 1024),),), (("g", 0, 288), ("s", 384, 512), ("s", 512, 896), ("s", 288, 384), ("s", 896, 1024), ("q", 384, 896), ("q", 0, 256), ("q", 256, 384), ("q", 896, 1024),)),
+    (4, (640,), (((0, 384),),), (("g", 0, 288), ("s", 384, 640), ("s", 288, 384), ("s", 640, 896), ("s", 896, 1024), ("q", 0, 256), ("q", 256, 384), ("q", 384, 896), ("q", 896, 1024),)),
 )
 
 
@@ -62,7 +61,6 @@ def tile_routed_moe_kernel(tc, xT, w_words, w_scales, b, gate, offs, out):
 
         slot_scales = [keep.tile([P, SLOTS], U8, name=f"slot_scales{g}", align_bytes=64) for g in range(len(PLANES_FROM))]
         slot_words = []
-        held_words = []
 
         def plane_of(a):
             g = len([start for start in PLANES_FROM if start <= a]) - 1
@@ -71,14 +69,13 @@ def tile_routed_moe_kernel(tc, xT, w_words, w_scales, b, gate, offs, out):
         def interleave(copy, grouped, raw):
             copy(grouped.rearrange("p (c i) t -> p c t i", i=4), raw.rearrange("p t (c i) -> p c t i", i=4))
 
-        held = None
         for a in range(PASSES):
             token_words = ring.tile([P, WINDOW], U32, name="token_words", align_bytes=64)
-            gathered = keep.tile([P, SLOTS if a == PASSES - 1 else SLOTS - HELD], U32, name=f"slot_words{a}", align_bytes=64)
+            gathered = keep.tile([P, SLOTS], U32, name=f"slot_words{a}", align_bytes=64)
             slot_words.append(gathered)
             g, first = plane_of(a)
 
-            late_rows, early, shared_ranges, copies, calls = PLAN[a]
+            late_rows, early, shared_ranges, steps = PLAN[a]
             if late_rows == 4:
                 cuts = (0,) + early + (T,)
                 parts = []
@@ -108,35 +105,33 @@ def tile_routed_moe_kernel(tc, xT, w_words, w_scales, b, gate, offs, out):
             def loaded(lo, hi):
                 return [part[:, :, lo - start:hi - start] for start, end, part in parts if start <= lo and hi <= end][0]
 
-            shared = single.tile([P, 768, 4], BF16, name="shared", align_bytes=64)
             others = ring.tile([P, T, 4], BF16, name="others", align_bytes=64)
+            shared = {}
 
             def grouped(lo, hi):
-                at = 0
-                for start, end in shared_ranges:
-                    if start <= lo and hi <= end:
-                        return shared[:, at + lo - start:at + hi - start, :]
-                    at += end - start
+                for ranges in shared_ranges:
+                    at = 0
+                    for start, end in ranges:
+                        if start <= lo and hi <= end:
+                            if ranges not in shared:
+                                shared[ranges] = single.tile([P, 512, 4], BF16, name="shared", align_bytes=64)
+                            return shared[ranges][:, at + lo - start:at + hi - start, :]
+                        at += end - start
                 return others[:, lo:hi, :]
 
-            for engine, lo, hi, t0, t1 in copies:
+            for engine, lo, hi in steps:
                 if engine == "g":
-                    nc.gpsimd.tensor_copy(grouped(lo, hi)[:, :, t0:t1], loaded(lo, hi)[:, t0:t1, :].rearrange("p t n -> p n t"))
+                    nc.gpsimd.tensor_copy(grouped(lo, hi), loaded(lo, hi).rearrange("p t n -> p n t"))
+                elif engine == "q":
+                    nc.vector.quantize_mx(
+                        out=token_words[:, lo:hi].bitcast(FP8X4),
+                        scales=token_scales[g][first:P, lo:hi],
+                        in_=grouped(lo, hi).rearrange("p n t -> p (n t)"),
+                    )
                 else:
-                    interleave(nc.vector.tensor_copy if engine == "v" else nc.scalar.copy, grouped(lo, hi)[:, :, t0:t1], loaded(lo, hi)[:, t0:t1, :])
-            for lo, hi in calls:
-                nc.vector.quantize_mx(
-                    out=token_words[:, lo:hi].bitcast(FP8X4),
-                    scales=token_scales[g][first:P, lo:hi],
-                    in_=grouped(lo, hi).rearrange("p n t -> p (n t)"),
-                )
-            if a > 0:
-                rest = keep.tile([P, HELD], U32, name=f"held_words{a}", tag=last_tag, align_bytes=64)
-                nc.vector.tensor_copy(rest[:], held[:, 0:T].indirect(entries(SLOTS - HELD, SLOTS)))
-                held_words.append(rest)
-            held = token_words
+                    interleave(nc.vector.tensor_copy if engine == "v" else nc.scalar.copy, grouped(lo, hi), loaded(lo, hi))
             if a < PASSES - 1:
-                nc.vector.tensor_copy(gathered[:], token_words[:].indirect(entries(0, SLOTS - HELD)))
+                nc.vector.tensor_copy(gathered[:], token_words[:].indirect(entries(0, SLOTS)))
                 if a == PLANES_FROM[1] - 1:
                     nc.vector.tensor_copy(slot_scales[0][:], token_scales[0][:].indirect(entries(0, SLOTS)))
             else:
@@ -179,11 +174,11 @@ def tile_routed_moe_kernel(tc, xT, w_words, w_scales, b, gate, offs, out):
                 features = slice(h * P, (h + 1) * P)
                 sums = psum.tile([P, C], F32, name=f"sums{e}{h}")
                 order = list(range(PASSES)) if e == 0 and h == 0 else list(reversed(range(PASSES)))
-                cuts = (slots.start, SLOTS - HELD, SLOTS) if e == E - 1 else (slots.start, slots.stop)
+                cuts = (slots.start, slots.stop)
                 for lo, hi in zip(cuts, cuts[1:]):
                     for a in order:
                         g, first = plane_of(a)
-                        words = held_words[a][:] if lo == SLOTS - HELD and a < PASSES - 1 else slot_words[a][:, lo:hi]
+                        words = slot_words[a][:, lo:hi]
                         nc.tensor.matmul_mx(
                             out=sums[:, lo - slots.start:hi - slots.start],
                             lhsT=weights[e][:, a, features].bitcast(FP8X4),

@@ -66,8 +66,8 @@ def tile_routed_moe_kernel(tc, xT, w_words, w_scales, b, gate, offs, out):
             g = len([start for start in PLANES_FROM if start <= a]) - 1
             return g, 4 * (a - PLANES_FROM[g])
 
-        def interleave(copy, grouped, raw):
-            copy(grouped.rearrange("p (c i) t -> p c t i", i=4), raw.rearrange("p t (c i) -> p c t i", i=4))
+        def interleave(copy, grouped, raw, run):
+            copy(grouped.rearrange("p (c i) t -> p c t i", i=run), raw.rearrange("p t (c i) -> p c t i", i=run))
 
         for a in range(PASSES):
             token_words = ring.tile([P, WINDOW], U32, name="token_words", align_bytes=64)
@@ -129,7 +129,7 @@ def tile_routed_moe_kernel(tc, xT, w_words, w_scales, b, gate, offs, out):
                         in_=grouped(lo, hi).rearrange("p n t -> p (n t)"),
                     )
                 else:
-                    interleave(nc.vector.tensor_copy if engine == "v" else nc.scalar.copy, grouped(lo, hi), loaded(lo, hi))
+                    interleave(nc.vector.tensor_copy if engine == "v" else nc.scalar.copy, grouped(lo, hi), loaded(lo, hi), 4 if engine == "v" else 2)
             if a < PASSES - 1:
                 nc.vector.tensor_copy(gathered[:], token_words[:].indirect(entries(0, SLOTS)))
                 if a == PLANES_FROM[1] - 1:

@@ -17,22 +17,20 @@ U32 = mybir.dt.uint32
 U16 = mybir.dt.uint16
 U8 = mybir.dt.uint8
 FP8X4 = mybir.dt.float8_e4m3fn_x4
+COPY = mybir.ActivationFunctionType.Copy
 RELU = mybir.ActivationFunctionType.Relu
 SQUARE = mybir.ActivationFunctionType.Square
+ADD = mybir.AluOpType.add
+MAX = mybir.AluOpType.max
 MULT = mybir.AluOpType.mult
 
 WINDOW = 1408
-
 PLANES_FROM = (0, 2)
-
-PLAN = (
-    (0, (3584,), (((512, 1024),),), (("v", 0, 384), ("s", 384, 512), ("v", 512, 768), ("s", 768, 1024), ("q", 0, 512), ("q", 512, 1024),)),
-    (0, (3584,), (((768, 1024),),), (("s", 0, 256), ("v", 256, 768), ("s", 768, 1024), ("q", 0, 256), ("q", 256, 768), ("q", 768, 1024),)),
-    (0, (3584,), (((0, 384), (896, 1024),),), (("g", 0, 288), ("s", 384, 512), ("s", 512, 896), ("s", 288, 384), ("s", 896, 1024), ("q", 384, 896), ("q", 0, 256), ("q", 256, 384), ("q", 896, 1024),)),
-    (0, (3584,), (((0, 384), (896, 1024),),), (("g", 0, 288), ("s", 384, 512), ("s", 512, 896), ("s", 288, 384), ("s", 896, 1024), ("q", 384, 896), ("q", 0, 256), ("q", 256, 384), ("q", 896, 1024),)),
-    (0, (3584,), (((0, 384), (896, 1024),),), (("g", 0, 288), ("s", 384, 512), ("s", 512, 896), ("s", 288, 384), ("s", 896, 1024), ("q", 384, 896), ("q", 0, 256), ("q", 256, 384), ("q", 896, 1024),)),
-    (4, (640,), (((0, 384),),), (("g", 0, 288), ("s", 384, 640), ("s", 288, 384), ("s", 640, 896), ("s", 896, 1024), ("q", 0, 256), ("q", 256, 384), ("q", 384, 896), ("q", 896, 1024),)),
-)
+HEAD_PASSES = 2
+EARLY = 512
+EARLY_LAST = 640
+POOL_TOKENS = 288
+HELD = 384
 
 
 def tile_routed_moe_kernel(tc, xT, w_words, w_scales, b, gate, offs, out):
@@ -66,39 +64,25 @@ def tile_routed_moe_kernel(tc, xT, w_words, w_scales, b, gate, offs, out):
             g = len([start for start in PLANES_FROM if start <= a]) - 1
             return g, 4 * (a - PLANES_FROM[g])
 
-        def interleave(copy, grouped, raw, run):
-            copy(grouped.rearrange("p (c i) t -> p c t i", i=run), raw.rearrange("p t (c i) -> p c t i", i=run))
-
         for a in range(PASSES):
+            last = a == PASSES - 1
             token_words = ring.tile([P, WINDOW], U32, name="token_words", align_bytes=64)
             gathered = keep.tile([P, SLOTS], U32, name=f"slot_words{a}", align_bytes=64)
             slot_words.append(gathered)
             g, first = plane_of(a)
 
-            late_rows, early, shared_ranges, steps = PLAN[a]
-            if late_rows == 4:
-                cuts = (0,) + early + (T,)
+            if last:
                 parts = []
-                for lo, hi in zip(cuts, cuts[1:]):
-                    last_tag = f"raw{a}_{lo}"
-                    part = keep.tile([P, 4, hi - lo], F32, name=last_tag, tag=last_tag, align_bytes=64)
+                for lo, hi in ((0, EARLY_LAST), (EARLY_LAST, T)):
+                    part = keep.tile([P, 4, hi - lo], F32, name=f"raw{a}_{lo}", align_bytes=64)
                     nc.sync.dma_start(out=part[:], in_=x_passes[a][:, :, lo:hi])
                     parts.append((lo, hi, part[:]))
             else:
-                last_tag = f"raw{a}"
-                raw = keep.tile([P, 4 * T], F32, name=last_tag, tag=last_tag, align_bytes=64)
-                rows = raw[:].rearrange("p (t n) -> p t n", t=4)
-                if late_rows == 0:
-                    cuts = (0,) + early + (4 * T,)
-                    for lo, hi in zip(cuts, cuts[1:]):
-                        nc.sync.dma_start(out=raw[:, lo:hi], in_=x_runs[a][:, lo:hi])
-                else:
-                    first_late = 4 - late_rows
-                    run = first_late * T + early
-                    nc.sync.dma_start(out=raw[:, 0:run], in_=x_runs[a][:, 0:run])
-                    nc.sync.dma_start(out=rows[:, first_late + 1:4, 0:early], in_=x_passes[a][:, first_late + 1:4, 0:early])
-                    nc.sync.dma_start(out=rows[:, first_late:4, early:T], in_=x_passes[a][:, first_late:4, early:T])
-                parts = [(0, T, rows)]
+                raw = keep.tile([P, 4 * T], F32, name=f"raw{a}", align_bytes=64)
+                cut = 3 * T + EARLY
+                for lo, hi in ((0, cut), (cut, 4 * T)):
+                    nc.sync.dma_start(out=raw[:, lo:hi], in_=x_runs[a][:, lo:hi])
+                parts = [(0, T, raw[:].rearrange("p (t n) -> p t n", t=4))]
             if a == 0:
                 nc.sync.dma_start(offsets[:], offs)
 
@@ -106,36 +90,79 @@ def tile_routed_moe_kernel(tc, xT, w_words, w_scales, b, gate, offs, out):
                 return [part[:, :, lo - start:hi - start] for start, end, part in parts if start <= lo and hi <= end][0]
 
             others = ring.tile([P, T, 4], BF16, name="others", align_bytes=64)
-            shared = {}
+            held = single.tile([P, 512, 4], BF16, name="held", align_bytes=64)
+            if a < HEAD_PASSES:
+                held_ranges = ((T - 512, T),) if a == 0 else ((T - 256, T),)
+            elif last:
+                held_ranges = ((0, HELD),)
+            else:
+                held_ranges = ((0, HELD), (T - 128, T))
 
             def grouped(lo, hi):
-                for ranges in shared_ranges:
-                    at = 0
-                    for start, end in ranges:
-                        if start <= lo and hi <= end:
-                            if ranges not in shared:
-                                shared[ranges] = single.tile([P, 512, 4], BF16, name="shared", align_bytes=64)
-                            return shared[ranges][:, at + lo - start:at + hi - start, :]
-                        at += end - start
+                at = 0
+                for start, end in held_ranges:
+                    if start <= lo and hi <= end:
+                        return held[:, at + lo - start:at + hi - start, :]
+                    at += end - start
                 return others[:, lo:hi, :]
 
-            for engine, lo, hi in steps:
-                if engine == "g":
-                    nc.gpsimd.tensor_copy(grouped(lo, hi), loaded(lo, hi).rearrange("p t n -> p n t"))
-                elif engine == "q":
-                    nc.vector.quantize_mx(
-                        out=token_words[:, lo:hi].bitcast(FP8X4),
-                        scales=token_scales[g][first:P, lo:hi],
-                        in_=grouped(lo, hi).rearrange("p n t -> p (n t)"),
-                    )
-                else:
-                    interleave(nc.vector.tensor_copy if engine == "v" else nc.scalar.copy, grouped(lo, hi), loaded(lo, hi), 4 if engine == "v" else 2)
-            if a < PASSES - 1:
+            def interleave(copy, lo, hi, run):
+                copy(
+                    grouped(lo, hi).rearrange("p (c i) t -> p c t i", i=run),
+                    loaded(lo, hi).rearrange("p t (c i) -> p c t i", i=run),
+                )
+
+            def on_vector(lo, hi):
+                interleave(nc.vector.tensor_copy, lo, hi, 4)
+
+            def on_scalar(lo, hi):
+                interleave(nc.scalar.copy, lo, hi, 2)
+
+            def quantise(lo, hi):
+                nc.vector.quantize_mx(
+                    out=token_words[:, lo:hi].bitcast(FP8X4),
+                    scales=token_scales[g][first:P, lo:hi],
+                    in_=grouped(lo, hi).rearrange("p n t -> p (n t)"),
+                )
+
+            if a == 1:
+                on_scalar(0, 256)
+                on_vector(256, 768)
+                on_scalar(768, T)
+                quantise(0, 256)
+                quantise(256, 768)
+                quantise(768, T)
+            elif a == 0:
+                on_vector(0, 384)
+                on_scalar(384, EARLY)
+                on_vector(EARLY, 768)
+                on_scalar(768, T)
+                quantise(0, EARLY)
+                quantise(EARLY, T)
+            else:
+                early = EARLY_LAST if last else EARLY
+                nc.gpsimd.tensor_copy(grouped(0, POOL_TOKENS), loaded(0, POOL_TOKENS).rearrange("p t n -> p n t"))
+                on_scalar(HELD, early)
+                if last:
+                    on_scalar(POOL_TOKENS, HELD)
+                on_scalar(early, T - 128)
+                if not last:
+                    on_scalar(POOL_TOKENS, HELD)
+                on_scalar(T - 128, T)
+                if not last:
+                    quantise(HELD, T - 128)
+                quantise(0, 256)
+                quantise(256, HELD)
+                if last:
+                    quantise(HELD, T - 128)
+                quantise(T - 128, T)
+
+            if not last:
                 nc.vector.tensor_copy(gathered[:], token_words[:].indirect(entries(0, SLOTS)))
                 if a == PLANES_FROM[1] - 1:
                     nc.vector.tensor_copy(slot_scales[0][:], token_scales[0][:].indirect(entries(0, SLOTS)))
             else:
-                for lo, hi in ((0, C), (C, SLOTS)):
+                for lo, hi in ((0, C), (C, 2 * C), (2 * C, SLOTS)):
                     nc.vector.tensor_copy(slot_scales[g][:, lo:hi], token_scales[g][:].indirect(entries(lo, hi)))
                     nc.vector.tensor_copy(gathered[:, lo:hi], token_words[:].indirect(entries(lo, hi)))
 
@@ -154,45 +181,65 @@ def tile_routed_moe_kernel(tc, xT, w_words, w_scales, b, gate, offs, out):
         weights = []
         bias = keep.tile([P, BLOCKS, E], F32, name="bias")
         gate_rows = keep.tile([P, SLOTS], F32, name="gate_rows")
+
+        def load_gate(e):
+            nc.sync.dma_start(out=gate_rows[:, e * C:(e + 1) * C], in_=gate[0:P, e * C:(e + 1) * C])
+
         for e in range(E):
-            codes = keep.tile([P, PASSES, N], U32, name=f"weights{e}", align_bytes=64)
+            codes = keep.tile([P, PASSES, N], U32, name=f"weights{e}", tag=f"weights{e}", align_bytes=64)
             nc.sync.dma_start(out=codes[:].bitcast(I32), in_=w_words[e].rearrange("a p n r -> p a (n r)").bitcast(I32))
             weights.append(codes)
             if e == 0:
                 nc.sync.dma_start(out=bias[:], in_=b.rearrange("(h p) e -> p h e", p=P))
-                nc.sync.dma_start(out=gate_rows[:, 0:C], in_=gate[0:P, 0:C])
-                load_scales(1, 2)
-            if e == 1:
-                nc.sync.dma_start(out=gate_rows[:, C:SLOTS], in_=gate[0:P, C:SLOTS])
-                load_scales(2, E)
+            load_gate(e)
+            if e < E - 1:
+                load_scales(e + 1, e + 2)
 
         results = [keep.tile([P, T], F32, name=f"results{h}") for h in range(BLOCKS)]
-        squares = [keep.tile([P, SLOTS], F32, name=f"squares{h}") for h in range(BLOCKS)]
-        for e in range(E):
+        positives = [keep.tile([P, SLOTS], F32, name=f"positives{h}") for h in range(BLOCKS)]
+        squares = keep.tile([P, SLOTS], F32, name="squares")
+        weighted = keep.tile([P, SLOTS], F32, name="weighted")
+
+        def prepare(e):
             slots = slice(e * C, (e + 1) * C)
-            for h in range(BLOCKS):
+            for h in ((1, 0) if e == 0 else (1, 0)):
                 features = slice(h * P, (h + 1) * P)
                 sums = psum.tile([P, C], F32, name=f"sums{e}{h}")
-                order = list(range(PASSES)) if e == 0 and h == 0 else list(reversed(range(PASSES)))
-                cuts = (slots.start, slots.stop)
-                for lo, hi in zip(cuts, cuts[1:]):
-                    for a in order:
-                        g, first = plane_of(a)
-                        words = slot_words[a][:, lo:hi]
-                        nc.tensor.matmul_mx(
-                            out=sums[:, lo - slots.start:hi - slots.start],
-                            lhsT=weights[e][:, a, features].bitcast(FP8X4),
-                            lhsT_scale=weight_scales[:, e * PASSES + a, features],
-                            rhs=words.bitcast(FP8X4),
-                            rhs_scale=slot_scales[g][first:P, lo:hi],
-                            start=(a == order[0]),
-                            stop=(a == order[-1]),
-                        )
-                positive = ring.tile([P, C], F32, name="positive")
-                nc.scalar.activation(positive[:], sums[:], RELU, bias=bias[:, h, e:e + 1])
-                nc.scalar.activation(squares[h][:, slots], positive[:], SQUARE)
-                nc.vector.tensor_tensor(
-                    results[h][:].indirect(entries(slots.start, slots.stop)), squares[h][:, slots], gate_rows[:, slots], MULT
-                )
-                if e == E - 1:
-                    nc.sync.dma_start(out=out[features, :], in_=results[h][:])
+                if e > 0:
+                    order = [2, 3, 4, 0, 1, 5]
+                else:
+                    order = [0, 1, 2, 3, 4, 5] if h == 1 else [0, 1, 5, 2, 3, 4]
+                for a in order:
+                    g, first = plane_of(a)
+                    nc.tensor.matmul_mx(
+                        out=sums[:],
+                        lhsT=weights[e][:, a, features].bitcast(FP8X4),
+                        lhsT_scale=weight_scales[:, e * PASSES + a, features],
+                        rhs=slot_words[a][:, slots].bitcast(FP8X4),
+                        rhs_scale=slot_scales[g][first:P, slots],
+                        start=(a == order[0]),
+                        stop=(a == order[-1]),
+                    )
+                nc.scalar.activation(positives[h][:, slots], sums[:], RELU, bias=bias[:, h, e:e + 1])
+                if h == 0:
+                    nc.vector.scalar_tensor_tensor(weighted[:, slots], sums[:], bias[:, h, e:e + 1], gate_rows[:, slots], ADD, MULT)
+            nc.scalar.activation(squares[:, slots], positives[1][:, slots], SQUARE)
+
+        def finish(e):
+            slots = slice(e * C, (e + 1) * C)
+            where = entries(slots.start, slots.stop)
+            tag = f"weights{e + 1}" if e in (1, 2) else f"gated{e}"
+            gated = keep.tile([P, C], F32, name=f"gated{e}", tag=tag, align_bytes=64)
+            nc.gpsimd.tensor_tensor(gated[:], squares[:, slots], gate_rows[:, slots], MULT)
+            nc.scalar.activation(results[1][:].indirect(where), gated[:], COPY)
+            nc.vector.tensor_tensor(results[0][:].indirect(where), positives[0][:, slots], weighted[:, slots], MULT)
+
+        prepare(0)
+        finish(0)
+        prepare(1)
+        for e in range(1, E):
+            if e + 1 < E:
+                prepare(e + 1)
+            finish(e)
+        nc.sync.dma_start(out=out[0:P, :], in_=results[0][:])
+        nc.scalar.dma_start(out=out[P:N, :], in_=results[1][:])

@@ -57,6 +57,11 @@ def tile_routed_moe_kernel(tc, xT, w_words, w_scales, b, gate, offs, out):
         weight_scales = keep.tile([P, E * PASSES, N], U8, name="weight_scales", align_bytes=64)
         nc.vector.memset(weight_scales[:].bitcast(I32), 0)
 
+        ones = keep.tile([P, P], F32, name="ones")
+        nc.vector.memset(ones[:], 1.0)
+        gate_row = keep.tile([P, SLOTS], F32, name="gate_row")
+        nc.vector.memset(gate_row[:], 0.0)
+
         slot_scales = [keep.tile([P, SLOTS], U8, name=f"slot_scales{g}", align_bytes=64) for g in range(len(PLANES_FROM))]
         slot_words = []
 
@@ -74,8 +79,10 @@ def tile_routed_moe_kernel(tc, xT, w_words, w_scales, b, gate, offs, out):
             if last:
                 parts = []
                 for lo, hi in ((0, EARLY_LAST), (EARLY_LAST, T)):
-                    part = keep.tile([P, 4, hi - lo], F32, name=f"raw{a}_{lo}", align_bytes=64)
+                    part = keep.tile([P, 4, hi - lo], F32, name=f"raw{a}_{lo}", tag=f"raw{a}_{lo}", align_bytes=64)
                     nc.sync.dma_start(out=part[:], in_=x_passes[a][:, :, lo:hi])
+                    if lo == 0:
+                        nc.sync.dma_start(out=gate_row[0:1, :], in_=gate[0:1, :])
                     parts.append((lo, hi, part[:]))
             else:
                 raw = keep.tile([P, 4 * T], F32, name=f"raw{a}", align_bytes=64)
@@ -162,9 +169,9 @@ def tile_routed_moe_kernel(tc, xT, w_words, w_scales, b, gate, offs, out):
                 if a == PLANES_FROM[1] - 1:
                     nc.vector.tensor_copy(slot_scales[0][:], token_scales[0][:].indirect(entries(0, SLOTS)))
             else:
-                for lo, hi in ((0, C), (C, 2 * C), (2 * C, SLOTS)):
-                    nc.vector.tensor_copy(slot_scales[g][:, lo:hi], token_scales[g][:].indirect(entries(lo, hi)))
-                    nc.vector.tensor_copy(gathered[:, lo:hi], token_words[:].indirect(entries(lo, hi)))
+                for lo, hi in ((0, C // 2), (C // 2, C), (C, 2 * C), (2 * C, 3 * C), (3 * C, SLOTS)):
+                    nc.vector.tensor_copy(slot_scales[g][:, lo:hi], token_scales[g][:, 0:T].indirect(entries(lo, hi)))
+                    nc.vector.tensor_copy(gathered[:, lo:hi], token_words[:, 0:T].indirect(entries(lo, hi)))
 
         scale_rows = w_scales.rearrange("e a q n -> q (e a) n")
 
@@ -176,22 +183,25 @@ def tile_routed_moe_kernel(tc, xT, w_words, w_scales, b, gate, offs, out):
                     in_=scale_rows[row:16:4, planes, :].bitcast(I32),
                 )
 
+        gate_rows = keep.tile([P, SLOTS], F32, name="gate_rows", tag=f"raw{PASSES - 1}_{EARLY_LAST}", align_bytes=64)
+        for h in range(BLOCKS):
+            columns = slice(h * 512, (h + 1) * 512)
+            spread = psum.tile([P, 512], F32, name=f"spread{h}", tag=f"bank{E - 1}{h}")
+            nc.tensor.matmul(spread[:], ones[:], gate_row[:, columns], start=True, stop=True)
+            nc.scalar.copy(gate_rows[:, columns], spread[:])
+
         load_scales(0, 1)
 
         weights = []
         bias = keep.tile([P, BLOCKS, E], F32, name="bias")
-        gate_rows = keep.tile([P, SLOTS], F32, name="gate_rows")
-
-        def load_gate(e):
-            nc.sync.dma_start(out=gate_rows[:, e * C:(e + 1) * C], in_=gate[0:P, e * C:(e + 1) * C])
-
         for e in range(E):
             codes = keep.tile([P, PASSES, N], U32, name=f"weights{e}", tag=f"weights{e}", align_bytes=64)
-            nc.sync.dma_start(out=codes[:].bitcast(I32), in_=w_words[e].rearrange("a p n r -> p a (n r)").bitcast(I32))
+            rows = w_words[e].rearrange("a p n r -> p a (n r)").bitcast(I32)
+            for lo, hi in (((0, 2), (2, PASSES)) if e == 0 else ((2, PASSES), (0, 2))):
+                nc.sync.dma_start(out=codes[:, lo:hi, :].bitcast(I32), in_=rows[:, lo:hi, :])
             weights.append(codes)
             if e == 0:
                 nc.sync.dma_start(out=bias[:], in_=b.rearrange("(h p) e -> p h e", p=P))
-            load_gate(e)
             if e < E - 1:
                 load_scales(e + 1, e + 2)
 
@@ -200,46 +210,78 @@ def tile_routed_moe_kernel(tc, xT, w_words, w_scales, b, gate, offs, out):
         squares = keep.tile([P, SLOTS], F32, name="squares")
         weighted = keep.tile([P, SLOTS], F32, name="weighted")
 
+        def open_sums(h, lo, hi, bank):
+            return psum.tile([P, hi - lo], F32, name=f"sums{h}_{lo}", tag=bank)
+
+        def passes(sums, h, lo, hi, order, start, stop):
+            e = lo // C
+            features = slice(h * P, (h + 1) * P)
+            for a in order:
+                g, first = plane_of(a)
+                nc.tensor.matmul_mx(
+                    out=sums[:],
+                    lhsT=weights[e][:, a, features].bitcast(FP8X4),
+                    lhsT_scale=weight_scales[:, e * PASSES + a, features],
+                    rhs=slot_words[a][:, lo:hi].bitcast(FP8X4),
+                    rhs_scale=slot_scales[g][first:P, lo:hi],
+                    start=(start and a == order[0]),
+                    stop=(stop and a == order[-1]),
+                )
+
+        def relu(sums, h, lo, hi):
+            e = lo // C
+            nc.scalar.activation(positives[h][:, lo:hi], sums[:], RELU, bias=bias[:, h, e:e + 1])
+
+        def multiply(h, lo, hi, order, bank):
+            sums = open_sums(h, lo, hi, bank)
+            passes(sums, h, lo, hi, order, True, True)
+            relu(sums, h, lo, hi)
+            return sums
+
+        def square(lo, hi):
+            nc.scalar.activation(squares[:, lo:hi], positives[1][:, lo:hi], SQUARE)
+
+        def weigh(e, sums):
+            slots = slice(e * C, (e + 1) * C)
+            nc.vector.scalar_tensor_tensor(weighted[:, slots], sums[:], bias[:, 0, e:e + 1], gate_rows[:, slots], ADD, MULT)
+
+        def scatter_second(lo, hi, tag):
+            gated = keep.tile([P, hi - lo], F32, name=f"gated{lo}", tag=tag, align_bytes=64)
+            nc.gpsimd.tensor_tensor(gated[:], squares[:, lo:hi], gate_rows[:, lo:hi], MULT)
+            nc.scalar.activation(results[1][:].indirect(entries(lo, hi)), gated[:], COPY)
+
+        def scatter_first(e):
+            slots = slice(e * C, (e + 1) * C)
+            nc.vector.tensor_tensor(results[0][:].indirect(entries(slots.start, slots.stop)), positives[0][:, slots], weighted[:, slots], MULT)
+
         def prepare(e):
-            slots = slice(e * C, (e + 1) * C)
-            for h in ((1, 0) if e == 0 else (1, 0)):
-                features = slice(h * P, (h + 1) * P)
-                sums = psum.tile([P, C], F32, name=f"sums{e}{h}")
-                if e > 0:
-                    order = [2, 3, 4, 0, 1, 5]
-                else:
-                    order = [0, 1, 2, 3, 4, 5] if h == 1 else [0, 1, 5, 2, 3, 4]
-                for a in order:
-                    g, first = plane_of(a)
-                    nc.tensor.matmul_mx(
-                        out=sums[:],
-                        lhsT=weights[e][:, a, features].bitcast(FP8X4),
-                        lhsT_scale=weight_scales[:, e * PASSES + a, features],
-                        rhs=slot_words[a][:, slots].bitcast(FP8X4),
-                        rhs_scale=slot_scales[g][first:P, slots],
-                        start=(a == order[0]),
-                        stop=(a == order[-1]),
-                    )
-                nc.scalar.activation(positives[h][:, slots], sums[:], RELU, bias=bias[:, h, e:e + 1])
-                if h == 0:
-                    nc.vector.scalar_tensor_tensor(weighted[:, slots], sums[:], bias[:, h, e:e + 1], gate_rows[:, slots], ADD, MULT)
-            nc.scalar.activation(squares[:, slots], positives[1][:, slots], SQUARE)
+            lo, hi = e * C, (e + 1) * C
+            sums = {h: open_sums(h, lo, hi, f"bank{e}{h}") for h in (1, 0)}
+            for h in (1, 0):
+                passes(sums[h], h, lo, hi, [2, 3, 4], True, False)
+            for h in (1, 0):
+                passes(sums[h], h, lo, hi, [5], False, False)
+            for h in (1, 0):
+                passes(sums[h], h, lo, hi, [0, 1], False, True)
+                relu(sums[h], h, lo, hi)
+            square(lo, hi)
+            weigh(e, sums[0])
 
-        def finish(e):
-            slots = slice(e * C, (e + 1) * C)
-            where = entries(slots.start, slots.stop)
-            tag = f"weights{e + 1}" if e in (1, 2) else f"gated{e}"
-            gated = keep.tile([P, C], F32, name=f"gated{e}", tag=tag, align_bytes=64)
-            nc.gpsimd.tensor_tensor(gated[:], squares[:, slots], gate_rows[:, slots], MULT)
-            nc.scalar.activation(results[1][:].indirect(where), gated[:], COPY)
-            nc.vector.tensor_tensor(results[0][:].indirect(where), positives[0][:, slots], weighted[:, slots], MULT)
-
-        prepare(0)
-        finish(0)
+        half = C // 2
+        multiply(1, 0, half, [0, 1, 2, 3, 4, 5], f"bank{E - 2}0")
+        square(0, half)
+        multiply(1, half, C, [0, 1, 2, 3, 4, 5], "bank01")
+        square(half, C)
+        scatter_second(0, half, "gated0")
+        multiply(0, 0, C, [5, 0, 1, 2, 3, 4], "bank00")
+        scatter_second(half, C, "gated0b")
+        nc.gpsimd.tensor_tensor(weighted[:, 0:C], positives[0][:, 0:C], gate_rows[:, 0:C], MULT)
+        scatter_first(0)
         prepare(1)
         for e in range(1, E):
             if e + 1 < E:
                 prepare(e + 1)
-            finish(e)
+            scatter_second(e * C, (e + 1) * C, f"weights{e + 1}" if e + 1 < E else "gated3")
+            scatter_first(e)
         nc.sync.dma_start(out=out[0:P, :], in_=results[0][:])
         nc.scalar.dma_start(out=out[P:N, :], in_=results[1][:])

@@ -169,7 +169,7 @@ def tile_routed_moe_kernel(tc, xT, w_words, w_scales, b, gate, offs, out):
                 if a == PLANES_FROM[1] - 1:
                     nc.vector.tensor_copy(slot_scales[0][:], token_scales[0][:].indirect(entries(0, SLOTS)))
             else:
-                for lo, hi in ((0, C // 2), (C // 2, C), (C, 2 * C), (2 * C, 3 * C), (3 * C, SLOTS)):
+                for lo, hi in ((0, C // 2), (C // 2, C), (C, 2 * C), (2 * C, SLOTS)):
                     nc.vector.tensor_copy(slot_scales[g][:, lo:hi], token_scales[g][:, 0:T].indirect(entries(lo, hi)))
                     nc.vector.tensor_copy(gathered[:, lo:hi], token_words[:, 0:T].indirect(entries(lo, hi)))
 
@@ -257,23 +257,31 @@ def tile_routed_moe_kernel(tc, xT, w_words, w_scales, b, gate, offs, out):
         def prepare(e):
             lo, hi = e * C, (e + 1) * C
             sums = {h: open_sums(h, lo, hi, f"bank{e}{h}") for h in (1, 0)}
+            groups = ([2, 3, 4], [0, 1], [5]) if e < E - 1 else ([2, 3, 4, 5], [0, 1])
+            for group in groups:
+                for h in (1, 0):
+                    passes(sums[h], h, lo, hi, group, group is groups[0], group is groups[-1])
             for h in (1, 0):
-                passes(sums[h], h, lo, hi, [2, 3, 4], True, False)
-            for h in (1, 0):
-                passes(sums[h], h, lo, hi, [5], False, False)
-            for h in (1, 0):
-                passes(sums[h], h, lo, hi, [0, 1], False, True)
                 relu(sums[h], h, lo, hi)
             square(lo, hi)
             weigh(e, sums[0])
 
         half = C // 2
-        multiply(1, 0, half, [0, 1, 2, 3, 4, 5], f"bank{E - 2}0")
+        low, high, first = open_sums(1, 0, half, f"bank{E - 2}0"), open_sums(1, half, C, "bank01"), open_sums(0, 0, C, "bank00")
+        passes(low, 1, 0, half, [0, 1], True, False)
+        passes(high, 1, half, C, [0, 1], True, False)
+        passes(first, 0, 0, C, [0, 1], True, False)
+        passes(low, 1, 0, half, [2, 3, 4, 5], False, True)
+        relu(low, 1, 0, half)
         square(0, half)
-        multiply(1, half, C, [0, 1, 2, 3, 4, 5], "bank01")
+        passes(high, 1, half, C, [2, 3, 4], False, False)
+        passes(first, 0, 0, C, [2, 3, 4], False, False)
+        passes(high, 1, half, C, [5], False, True)
+        passes(first, 0, 0, C, [5], False, True)
+        relu(high, 1, half, C)
         square(half, C)
         scatter_second(0, half, "gated0")
-        multiply(0, 0, C, [5, 0, 1, 2, 3, 4], "bank00")
+        relu(first, 0, 0, C)
         scatter_second(half, C, "gated0b")
         nc.gpsimd.tensor_tensor(weighted[:, 0:C], positives[0][:, 0:C], gate_rows[:, 0:C], MULT)
         scatter_first(0)

@@ -64,6 +64,7 @@ def tile_routed_moe_kernel(tc, xT, w_words, w_scales, b, gate, offs, out):
 
         slot_scales = [keep.tile([P, SLOTS], U8, name=f"slot_scales{g}", align_bytes=64) for g in range(len(PLANES_FROM))]
         slot_words = []
+        last_words = {}
 
         def plane_of(a):
             g = len([start for start in PLANES_FROM if start <= a]) - 1
@@ -72,7 +73,7 @@ def tile_routed_moe_kernel(tc, xT, w_words, w_scales, b, gate, offs, out):
         for a in range(PASSES):
             last = a == PASSES - 1
             token_words = ring.tile([P, WINDOW], U32, name="token_words", align_bytes=64)
-            gathered = keep.tile([P, SLOTS], U32, name=f"slot_words{a}", align_bytes=64)
+            gathered = keep.tile([P, 2 * C if last else SLOTS], U32, name=f"slot_words{a}", align_bytes=64)
             slot_words.append(gathered)
             g, first = plane_of(a)
 
@@ -169,9 +170,13 @@ def tile_routed_moe_kernel(tc, xT, w_words, w_scales, b, gate, offs, out):
                 if a == PLANES_FROM[1] - 1:
                     nc.vector.tensor_copy(slot_scales[0][:], token_scales[0][:].indirect(entries(0, SLOTS)))
             else:
-                for lo, hi in ((0, C // 2), (C // 2, C), (C, 2 * C), (2 * C, SLOTS)):
+                for lo, hi in ((0, C // 2), (C // 2, C), (C, 2 * C)):
                     nc.vector.tensor_copy(slot_scales[g][:, lo:hi], token_scales[g][:, 0:T].indirect(entries(lo, hi)))
                     nc.vector.tensor_copy(gathered[:, lo:hi], token_words[:, 0:T].indirect(entries(lo, hi)))
+                nc.vector.tensor_copy(slot_scales[g][:, 2 * C:SLOTS], token_scales[g][:, 0:T].indirect(entries(2 * C, SLOTS)))
+                for e in range(2, E):
+                    last_words[e] = keep.tile([P, C], U32, name=f"last_words{e}", tag=f"last_words{e}", align_bytes=64)
+                    nc.vector.tensor_copy(last_words[e][:], token_words[:, 0:T].indirect(entries(e * C, (e + 1) * C)))
 
         scale_rows = w_scales.rearrange("e a q n -> q (e a) n")
 
@@ -222,7 +227,7 @@ def tile_routed_moe_kernel(tc, xT, w_words, w_scales, b, gate, offs, out):
                     out=sums[:],
                     lhsT=weights[e][:, a, features].bitcast(FP8X4),
                     lhsT_scale=weight_scales[:, e * PASSES + a, features],
-                    rhs=slot_words[a][:, lo:hi].bitcast(FP8X4),
+                    rhs=(last_words[e][:] if a == PASSES - 1 and e in last_words else slot_words[a][:, lo:hi]).bitcast(FP8X4),
                     rhs_scale=slot_scales[g][first:P, lo:hi],
                     start=(start and a == order[0]),
                     stop=(stop and a == order[-1]),
@@ -257,11 +262,14 @@ def tile_routed_moe_kernel(tc, xT, w_words, w_scales, b, gate, offs, out):
         def prepare(e):
             lo, hi = e * C, (e + 1) * C
             sums = {h: open_sums(h, lo, hi, f"bank{e}{h}") for h in (1, 0)}
-            groups = ([2, 3, 4], [0, 1], [5]) if e < E - 1 else ([2, 3, 4, 5], [0, 1])
-            for group in groups:
-                for h in (1, 0):
-                    passes(sums[h], h, lo, hi, group, group is groups[0], group is groups[-1])
-            for h in (1, 0):
+            if e == 1:
+                for group in ([2, 3, 4], [0, 1], [5]):
+                    for h in (0, 1):
+                        passes(sums[h], h, lo, hi, group, group[0] == 2, group[0] == 5)
+            else:
+                passes(sums[1], 1, lo, hi, [2, 3, 4, 0, 1, 5], True, True)
+                passes(sums[0], 0, lo, hi, [2, 3, 4, 5, 0, 1], True, True)
+            for h in ((0, 1) if e == 1 else (1, 0)):
                 relu(sums[h], h, lo, hi)
             square(lo, hi)
             weigh(e, sums[0])
@@ -279,17 +287,17 @@ def tile_routed_moe_kernel(tc, xT, w_words, w_scales, b, gate, offs, out):
         passes(high, 1, half, C, [5], False, True)
         passes(first, 0, 0, C, [5], False, True)
         relu(high, 1, half, C)
+        relu(first, 0, 0, C)
         square(half, C)
         scatter_second(0, half, "gated0")
-        relu(first, 0, 0, C)
-        scatter_second(half, C, "gated0b")
         nc.gpsimd.tensor_tensor(weighted[:, 0:C], positives[0][:, 0:C], gate_rows[:, 0:C], MULT)
+        scatter_second(half, C, "gated0b")
         scatter_first(0)
         prepare(1)
         for e in range(1, E):
             if e + 1 < E:
                 prepare(e + 1)
-            scatter_second(e * C, (e + 1) * C, f"weights{e + 1}" if e + 1 < E else "gated3")
+            scatter_second(e * C, (e + 1) * C, f"last_words{e + 1}" if e + 1 < E else "gated3")
             scatter_first(e)
         nc.sync.dma_start(out=out[0:P, :], in_=results[0][:])
         nc.scalar.dma_start(out=out[P:N, :], in_=results[1][:])

@@ -88,7 +88,7 @@ def tile_routed_moe_kernel(tc, xT, w_words, w_scales, b, gate, offs, out):
             else:
                 raw = keep.tile([P, 4 * T], F32, name=f"raw{a}", align_bytes=64)
                 cut = 3 * T + EARLY
-                for lo, hi in ((0, cut), (cut, 4 * T)):
+                for lo, hi in (((0, 4 * T),) if a in (2, 3) else ((0, cut), (cut, 4 * T))):
                     nc.sync.dma_start(out=raw[:, lo:hi], in_=x_runs[a][:, lo:hi])
                 parts = [(0, T, raw[:].rearrange("p (t n) -> p t n", t=4))]
             if a == 0:
@@ -134,8 +134,9 @@ def tile_routed_moe_kernel(tc, xT, w_words, w_scales, b, gate, offs, out):
                 )
 
             if a == 1:
-                on_scalar(0, 256)
-                on_vector(256, 768)
+                nc.gpsimd.tensor_copy(grouped(0, 128), loaded(0, 128).rearrange("p t n -> p n t"))
+                on_scalar(128, 384)
+                on_vector(384, 768)
                 on_scalar(768, T)
                 quantise(0, 256)
                 quantise(256, 768)

from contextlib import ExitStack

import concourse.mybir as mybir

K, T, E, C, N = 3072, 1024, 4, 256, 256
P = 128
PASSES = K // 512
SLOTS = E * C
BLOCKS = N // P
FLOPS = 2 * K * N * SLOTS
BYTES = 4 * K * T + E * K * N + E * K * N // 32 + 4 * N * E + 4 * SLOTS + 2 * P * (SLOTS // 16) + 4 * N * T

F32 = mybir.dt.float32
BF16 = mybir.dt.bfloat16
I32 = mybir.dt.int32
U32 = mybir.dt.uint32
U16 = mybir.dt.uint16
U8 = mybir.dt.uint8
FP8X4 = mybir.dt.float8_e4m3fn_x4
COPY = mybir.ActivationFunctionType.Copy
RELU = mybir.ActivationFunctionType.Relu
SQUARE = mybir.ActivationFunctionType.Square
ADD = mybir.AluOpType.add
MAX = mybir.AluOpType.max
MULT = mybir.AluOpType.mult

WINDOW = 1408
PLANES_FROM = (0, 2)
HEAD_PASSES = 2
EARLY = 512
EARLY_LAST = 640
POOL_TOKENS = 288
HELD = 384


def tile_routed_moe_kernel(tc, xT, w_words, w_scales, b, gate, offs, out):
    nc = tc.nc
    x_passes = xT.rearrange("(a p t) n -> a p t n", p=P, t=4)
    x_runs = xT.rearrange("(a p t) n -> a p (t n)", p=P, t=4)

    with ExitStack() as ctx:
        keep = ctx.enter_context(tc.tile_pool(name="keep", bufs=1))
        ring = ctx.enter_context(tc.tile_pool(name="ring", bufs=3))
        single = ctx.enter_context(tc.tile_pool(name="single", bufs=1))
        psum = ctx.enter_context(tc.psum_pool(name="psum", bufs=1))

        offsets = keep.tile([P, SLOTS // 16], U16, name="offsets")

        def entries(lo, hi):
            return offsets[:, lo // 16:hi // 16]

        token_scales = []
        for g in range(len(PLANES_FROM)):
            planes = keep.tile([P, WINDOW], U8, name=f"token_scales{g}", align_bytes=64)
            nc.vector.memset(planes[:, 0:T].bitcast(I32), 0)
            token_scales.append(planes)
        weight_scales = keep.tile([P, E * PASSES, N], U8, name="weight_scales", align_bytes=64)
        nc.vector.memset(weight_scales[:].bitcast(I32), 0)

        ones = keep.tile([P, P], F32, name="ones")
        nc.vector.memset(ones[:], 1.0)
        gate_row = keep.tile([P, SLOTS], F32, name="gate_row")
        nc.vector.memset(gate_row[:], 0.0)

        slot_scales = [keep.tile([P, SLOTS], U8, name=f"slot_scales{g}", align_bytes=64) for g in range(len(PLANES_FROM))]
        slot_words = []
        last_words = {}

        def plane_of(a):
            g = len([start for start in PLANES_FROM if start <= a]) - 1
            return g, 4 * (a - PLANES_FROM[g])

        for a in range(PASSES):
            last = a == PASSES - 1
            token_words = ring.tile([P, WINDOW], U32, name="token_words", align_bytes=64)
            gathered = keep.tile([P, 2 * C if last else SLOTS], U32, name=f"slot_words{a}", align_bytes=64)
            slot_words.append(gathered)
            g, first = plane_of(a)

            if last:
                parts = []
                for lo, hi in ((0, EARLY_LAST), (EARLY_LAST, T)):
                    part = keep.tile([P, 4, hi - lo], F32, name=f"raw{a}_{lo}", tag=f"raw{a}_{lo}", align_bytes=64)
                    nc.sync.dma_start(out=part[:], in_=x_passes[a][:, :, lo:hi])
                    if lo == 0:
                        nc.sync.dma_start(out=gate_row[0:1, :], in_=gate[0:1, :])
                    parts.append((lo, hi, part[:]))
            else:
                raw = keep.tile([P, 4 * T], F32, name=f"raw{a}", align_bytes=64)
                cut = 3 * T + EARLY
                for lo, hi in (((0, 4 * T),) if a in (2, 3) else ((0, cut), (cut, 4 * T))):
                    nc.sync.dma_start(out=raw[:, lo:hi], in_=x_runs[a][:, lo:hi])
                parts = [(0, T, raw[:].rearrange("p (t n) -> p t n", t=4))]
            if a == 0:
                nc.sync.dma_start(offsets[:], offs)

            def loaded(lo, hi):
                return [part[:, :, lo - start:hi - start] for start, end, part in parts if start <= lo and hi <= end][0]

            others = ring.tile([P, T, 4], BF16, name="others", align_bytes=64)
            held = single.tile([P, 512, 4], BF16, name="held", align_bytes=64)
            if a < HEAD_PASSES:
                held_ranges = ((T - 512, T),) if a == 0 else ((T - 256, T),)
            elif last:
                held_ranges = ((0, HELD),)
            else:
                held_ranges = ((0, HELD), (T - 128, T))

            def grouped(lo, hi):
                at = 0
                for start, end in held_ranges:
                    if start <= lo and hi <= end:
                        return held[:, at + lo - start:at + hi - start, :]
                    at += end - start
                return others[:, lo:hi, :]

            def interleave(copy, lo, hi, run):
                copy(
                    grouped(lo, hi).rearrange("p (c i) t -> p c t i", i=run),
                    loaded(lo, hi).rearrange("p t (c i) -> p c t i", i=run),
                )

            def on_vector(lo, hi):
                interleave(nc.vector.tensor_copy, lo, hi, 4)

            def on_scalar(lo, hi):
                interleave(nc.scalar.copy, lo, hi, 2)

            def quantise(lo, hi):
                nc.vector.quantize_mx(
                    out=token_words[:, lo:hi].bitcast(FP8X4),
                    scales=token_scales[g][first:P, lo:hi],
                    in_=grouped(lo, hi).rearrange("p n t -> p (n t)"),
                )

            if a == 1:
                nc.gpsimd.tensor_copy(grouped(0, 128), loaded(0, 128).rearrange("p t n -> p n t"))
                on_scalar(128, 384)
                on_vector(384, 768)
                on_scalar(768, T)
                quantise(0, 256)
                quantise(256, 768)
                quantise(768, T)
            elif a == 0:
                on_vector(0, 384)
                on_scalar(384, EARLY)
                on_vector(EARLY, 768)
                on_scalar(768, T)
                quantise(0, EARLY)
                quantise(EARLY, T)
            else:
                early = EARLY_LAST if last else EARLY
                nc.gpsimd.tensor_copy(grouped(0, POOL_TOKENS), loaded(0, POOL_TOKENS).rearrange("p t n -> p n t"))
                on_scalar(HELD, early)
                if last:
                    on_scalar(POOL_TOKENS, HELD)
                on_scalar(early, T - 128)
                if not last:
                    on_scalar(POOL_TOKENS, HELD)
                on_scalar(T - 128, T)
                if not last:
                    quantise(HELD, T - 128)
                quantise(0, 256)
                quantise(256, HELD)
                if last:
                    quantise(HELD, T - 128)
                quantise(T - 128, T)

            if not last:
                nc.vector.tensor_copy(gathered[:], token_words[:].indirect(entries(0, SLOTS)))
                if a == PLANES_FROM[1] - 1:
                    nc.vector.tensor_copy(slot_scales[0][:], token_scales[0][:].indirect(entries(0, SLOTS)))
            else:
                for lo, hi in ((0, C // 2), (C // 2, C), (C, 2 * C)):
                    nc.vector.tensor_copy(slot_scales[g][:, lo:hi], token_scales[g][:, 0:T].indirect(entries(lo, hi)))
                    nc.vector.tensor_copy(gathered[:, lo:hi], token_words[:, 0:T].indirect(entries(lo, hi)))
                nc.vector.tensor_copy(slot_scales[g][:, 2 * C:SLOTS], token_scales[g][:, 0:T].indirect(entries(2 * C, SLOTS)))
                for e in range(2, E):
                    last_words[e] = keep.tile([P, C], U32, name=f"last_words{e}", tag=f"last_words{e}", align_bytes=64)
                    nc.vector.tensor_copy(last_words[e][:], token_words[:, 0:T].indirect(entries(e * C, (e + 1) * C)))

        scale_rows = w_scales.rearrange("e a q n -> q (e a) n")

        def load_scales(first_expert, end_expert):
            planes = slice(first_expert * PASSES, end_expert * PASSES)
            for row in range(4):
                nc.sync.dma_start(
                    out=weight_scales[row:P:32, planes, :].bitcast(I32),
                    in_=scale_rows[row:16:4, planes, :].bitcast(I32),
                )

        gate_rows = keep.tile([P, SLOTS], F32, name="gate_rows", tag=f"raw{PASSES - 1}_{EARLY_LAST}", align_bytes=64)
        for h in range(BLOCKS):
            columns = slice(h * 512, (h + 1) * 512)
            spread = psum.tile([P, 512], F32, name=f"spread{h}", tag=f"bank{E - 1}{h}")
            nc.tensor.matmul(spread[:], ones[:], gate_row[:, columns], start=True, stop=True)
            nc.scalar.copy(gate_rows[:, columns], spread[:])

        load_scales(0, 1)

        weights = []
        bias = keep.tile([P, BLOCKS, E], F32, name="bias")
        for e in range(E):
            codes = keep.tile([P, PASSES, N], U32, name=f"weights{e}", tag=f"weights{e}", align_bytes=64)
            rows = w_words[e].rearrange("a p n r -> p a (n r)").bitcast(I32)
            for lo, hi in (((0, 2), (2, PASSES)) if e == 0 else ((2, PASSES), (0, 2))):
                nc.sync.dma_start(out=codes[:, lo:hi, :].bitcast(I32), in_=rows[:, lo:hi, :])
            weights.append(codes)
            if e == 0:
                nc.sync.dma_start(out=bias[:], in_=b.rearrange("(h p) e -> p h e", p=P))
            if e < E - 1:
                load_scales(e + 1, e + 2)

        results = [keep.tile([P, T], F32, name=f"results{h}") for h in range(BLOCKS)]
        positives = [keep.tile([P, SLOTS], F32, name=f"positives{h}") for h in range(BLOCKS)]
        squares = keep.tile([P, SLOTS], F32, name="squares")
        weighted = keep.tile([P, SLOTS], F32, name="weighted")

        def open_sums(h, lo, hi, bank):
            return psum.tile([P, hi - lo], F32, name=f"sums{h}_{lo}", tag=bank)

        def passes(sums, h, lo, hi, order, start, stop):
            e = lo // C
            features = slice(h * P, (h + 1) * P)
            for a in order:
                g, first = plane_of(a)
                nc.tensor.matmul_mx(
                    out=sums[:],
                    lhsT=weights[e][:, a, features].bitcast(FP8X4),
                    lhsT_scale=weight_scales[:, e * PASSES + a, features],
                    rhs=(last_words[e][:] if a == PASSES - 1 and e in last_words else slot_words[a][:, lo:hi]).bitcast(FP8X4),
                    rhs_scale=slot_scales[g][first:P, lo:hi],
                    start=(start and a == order[0]),
                    stop=(stop and a == order[-1]),
                )

        def relu(sums, h, lo, hi):
            e = lo // C
            nc.scalar.activation(positives[h][:, lo:hi], sums[:], RELU, bias=bias[:, h, e:e + 1])

        def multiply(h, lo, hi, order, bank):
            sums = open_sums(h, lo, hi, bank)
            passes(sums, h, lo, hi, order, True, True)
            relu(sums, h, lo, hi)
            return sums

        def square(lo, hi):
            nc.scalar.activation(squares[:, lo:hi], positives[1][:, lo:hi], SQUARE)

        def weigh(e, sums):
            slots = slice(e * C, (e + 1) * C)
            nc.vector.scalar_tensor_tensor(weighted[:, slots], sums[:], bias[:, 0, e:e + 1], gate_rows[:, slots], ADD, MULT)

        def scatter_second(lo, hi, tag):
            gated = keep.tile([P, hi - lo], F32, name=f"gated{lo}", tag=tag, align_bytes=64)
            nc.gpsimd.tensor_tensor(gated[:], squares[:, lo:hi], gate_rows[:, lo:hi], MULT)
            nc.scalar.activation(results[1][:].indirect(entries(lo, hi)), gated[:], COPY)

        def scatter_first(e):
            slots = slice(e * C, (e + 1) * C)
            nc.vector.tensor_tensor(results[0][:].indirect(entries(slots.start, slots.stop)), positives[0][:, slots], weighted[:, slots], MULT)

        def prepare(e):
            lo, hi = e * C, (e + 1) * C
            sums = {h: open_sums(h, lo, hi, f"bank{e}{h}") for h in (1, 0)}
            if e == 1:
                for group in ([2, 3, 4], [0, 1], [5]):
                    for h in (0, 1):
                        passes(sums[h], h, lo, hi, group, group[0] == 2, group[0] == 5)
            else:
                passes(sums[1], 1, lo, hi, [2, 3, 4, 0, 1, 5], True, True)
                passes(sums[0], 0, lo, hi, [2, 3, 4, 5, 0, 1], True, True)
            for h in ((0, 1) if e == 1 else (1, 0)):
                relu(sums[h], h, lo, hi)
            square(lo, hi)
            weigh(e, sums[0])

        half = C // 2
        low, high, first = open_sums(1, 0, half, f"bank{E - 2}0"), open_sums(1, half, C, "bank01"), open_sums(0, 0, C, "bank00")
        passes(low, 1, 0, half, [0, 1], True, False)
        passes(high, 1, half, C, [0, 1], True, False)
        passes(first, 0, 0, C, [0, 1], True, False)
        passes(low, 1, 0, half, [2, 3, 4, 5], False, True)
        relu(low, 1, 0, half)
        square(0, half)
        passes(high, 1, half, C, [2, 3, 4], False, False)
        passes(first, 0, 0, C, [2, 3, 4], False, False)
        passes(high, 1, half, C, [5], False, True)
        passes(first, 0, 0, C, [5], False, True)
        relu(high, 1, half, C)
        relu(first, 0, 0, C)
        square(half, C)
        scatter_second(0, half, "gated0")
        nc.gpsimd.tensor_tensor(weighted[:, 0:C], positives[0][:, 0:C], gate_rows[:, 0:C], MULT)
        scatter_second(half, C, "gated0b")
        scatter_first(0)
        prepare(1)
        for e in range(1, E):
            if e + 1 < E:
                prepare(e + 1)
            scatter_second(e * C, (e + 1) * C, f"last_words{e + 1}" if e + 1 < E else "gated3")
            scatter_first(e)
        nc.sync.dma_start(out=out[0:P, :], in_=results[0][:])
        nc.scalar.dma_start(out=out[P:N, :], in_=results[1][:])
